import numpy as np
import ml_dtypes


def mxq(x, axis, fmt="e4m3"):
    dtype, down = {"e4m3": (ml_dtypes.float8_e4m3fn, 7), "e5m2": (ml_dtypes.float8_e5m2, 14)}[fmt]
    v = np.moveaxis(np.asarray(x, np.float32).astype(ml_dtypes.bfloat16).astype(np.float64), axis, -1)
    blocks = v.reshape(v.shape[:-1] + (-1, 32))
    amax = np.abs(blocks).max(-1, keepdims=True)
    byte = np.maximum(np.where(amax > 0, np.frexp(amax)[1] - 1 + 127, 0) - down, 1)
    scale = np.exp2(byte - 127.0)
    codes = (blocks / scale).astype(np.float32).astype(dtype).astype(np.float64)
    return np.moveaxis((codes * scale).reshape(v.shape), -1, axis)


WIDE = False


def mx_kscale(k):
    if not WIDE:
        return np.ones(k)
    levels = np.array([10, -10, 5, -5, 0])
    if k % 512:
        return np.exp2(np.random.permutation(np.resize(levels, k // 32))).repeat(32)
    a = np.empty((k // 512, 16))
    for p in range(k // 512):
        a[p, :8] = np.random.permutation(np.resize(levels, 8))
        for g in range(8):
            far = levels[np.abs(levels - a[p, g]) >= 10]
            a[p, g + 8] = far[np.random.randint(len(far))]
    return np.exp2(a.ravel()).repeat(32)


def f64(x):
    return np.asarray(x).astype(np.float64)


def striped(idx):
    return np.tile(idx.reshape(-1, 16).T, (8, 1)).astype(np.uint16)


def unstriped(offs):
    return offs[:16].T.reshape(-1).astype(np.int64)


def pack_weight(w):
    k, n = w.shape
    w = f64(np.asarray(w, np.float32).astype(ml_dtypes.bfloat16)).reshape(k // 32, 32, n)
    amax = np.abs(w).max(1)
    byte = np.clip(np.where(amax > 0, np.frexp(amax)[1] - 1 + 127 - 7, 1), 1, 254)
    scaled = (w * np.exp2(127.0 - byte)[:, None, :]).reshape(k, n).astype(np.float32)
    words = np.ascontiguousarray(scaled.reshape(k // 512, 128, 4, n).transpose(0, 1, 3, 2)).astype(ml_dtypes.float8_e4m3fn).view(np.uint8)
    return words, np.ascontiguousarray(byte.astype(np.uint8).reshape(k // 512, 16, n))


def unpack_weight(words, scales):
    g, p, n, _ = words.shape
    vals = np.ascontiguousarray(words).view(ml_dtypes.float8_e4m3fn).astype(np.float64) * np.repeat(np.exp2(scales.astype(np.float64) - 127.0), 8, axis=1)[..., None]
    return vals.transpose(0, 1, 3, 2).reshape(g * 512, n)


def gelu(v):
    return 0.5 * v * (1.0 + np.tanh(np.sqrt(2.0 / np.pi) * (v + 0.044715 * v**3)))


K, T, S, H, N, U = 1024, 2048, 512, 512, 128, 1024


def setup_inputs():
    n = np.random.standard_normal
    s = mx_kscale(K)[:, None]
    u = mx_kscale(H)
    packed_xT = pack_weight(n((K, T)) * s)
    packed_w2 = pack_weight(n((H, N)) / np.sqrt(H) / u[:, None])
    return {
        "x_words": packed_xT[0],
        "x_scales": packed_xT[1],
        "w1": (n((K, H)) / np.sqrt(K) / s * u).astype(np.float32),
        "w2_words": packed_w2[0],
        "w2_scales": packed_w2[1],
        "skip": (n((H, U)) * u[:, None]).astype(np.float32),
        "offs": striped(np.random.permutation(T)[:S]),
        "cell": striped(np.random.permutation(U)[:S]),
    }


def reference(x_words, x_scales, w1, w2_words, w2_scales, skip, offs, cell):
    xq = unpack_weight(x_words, x_scales)[:, unstriped(offs)]
    up = np.zeros((H, U))
    up[:, unstriped(cell)] = gelu(mxq(f64(w1), 0, "e4m3").T @ xq)
    z = up + f64(skip)
    return unpack_weight(w2_words, w2_scales).T @ mxq(z, 0, "e4m3")

@@ -1,0 +1,165 @@
+from contextlib import ExitStack
+
+import concourse.mybir as mybir
+
+K, T, S, H, N, U = 1024, 2048, 512, 512, 128, 1024
+FLOPS = 2 * K * H * S + 2 * H * N * U
+
+F32 = mybir.dt.float32
+BF16 = mybir.dt.bfloat16
+I32 = mybir.dt.int32
+U32 = mybir.dt.uint32
+U16 = mybir.dt.uint16
+U8 = mybir.dt.uint8
+FP8X4 = mybir.dt.float8_e4m3fn_x4
+GELU = mybir.ActivationFunctionType.Gelu_apprx_tanh
+ADD = mybir.AluOpType.add
+
+P = 128
+PACK = 4
+K_PASS = P * PACK
+PASSES = K // K_PASS
+LIST_ROWS = 16
+CELL_PIECES = [(0, 256), (512, 1024), (256, 512)]
+
+
+def tile_picked_unet_gelu_p_kernel(
+    tc, x_words, x_scales, w1, w2_words, w2_scales, skip, offs, cell, out
+):
+    nc = tc.nc
+    with ExitStack() as ctx:
+        keep = ctx.enter_context(tc.tile_pool(name="keep", bufs=1))
+        psum = ctx.enter_context(tc.psum_pool(name="psum", bufs=1))
+
+        def sb(name, shape, dtype, tag=None):
+            return keep.tile(shape, dtype, name=name, tag=tag or name, align_bytes=64)
+
+        offs_sb = keep.tile([P, S // LIST_ROWS], U16, name="offs_sb")
+        cell_sb = keep.tile([P, S // LIST_ROWS], U16, name="cell_sb")
+
+        warm = sb("warm", [P, 16], F32)
+        nc.vector.memset(warm[:, 0:8], 0.0)
+        x_scale_table = sb("x_scale_table", [P, T], U8)
+        nc.vector.memset(x_scale_table[:].bitcast(I32), 0)
+        nc.scalar.activation(warm[:, 8:16], warm[:, 0:8], GELU)
+
+        nc.sync.dma_start(offs_sb[:], offs)
+        w1_raw, x_table = [], []
+        for g in range(PASSES):
+            raw = sb("w1_raw%d" % g, [P, PACK, H], F32)
+            nc.sync.dma_start(out=raw[:], in_=w1[g * K_PASS : (g + 1) * K_PASS, :].rearrange("(p j) c -> p j c", j=PACK))
+            w1_raw.append(raw)
+            table = sb("x_table%d" % g, [P, T], I32)
+            nc.sync.dma_start(out=table[:], in_=x_words[g].rearrange("p n t -> p (n t)").bitcast(I32))
+            x_table.append(table)
+            for r in range(4):
+                nc.scalar.dma_start(
+                    out=x_scale_table[4 * g + r : P : 32, :].bitcast(I32), in_=x_scales[g, r:16:4, :].bitcast(I32)
+                )
+        nc.sync.dma_start(cell_sb[:], cell)
+        skip_rows = skip.rearrange("(p t) v -> t p v", t=PACK)
+        skip_sb = []
+        for t in range(PACK):
+            plane = sb("skip%d" % t, [P, U], F32)
+            nc.sync.dma_start(out=plane[:], in_=skip_rows[t])
+            skip_sb.append(plane)
+        w2_codes = sb("w2_codes", [P, N], I32)
+        nc.sync.dma_start(out=w2_codes[:], in_=w2_words[0].rearrange("p n t -> p (n t)").bitcast(I32))
+        w2_plane = sb("w2_plane", [P, N], U8)
+        nc.vector.memset(w2_plane[:].bitcast(I32), 0)
+        for r in range(4):
+            nc.sync.dma_start(out=w2_plane[r:P:32, :].bitcast(I32), in_=w2_scales[0, r:16:4, :].bitcast(I32))
+
+        up = []
+        for t in range(PACK):
+            window = sb("up%d" % t, [P, U], F32)
+            nc.vector.memset(window[:], 0.0)
+            up.append(window)
+
+        x_plane = sb("x_plane", [P, S], U8)
+        nc.vector.tensor_copy(x_plane[:], x_scale_table[:].indirect(offs_sb[:]))
+
+        half = S // 2
+        halves = [slice(0, half), slice(half, S)]
+        list_halves = [slice(0, half // LIST_ROWS), slice(half // LIST_ROWS, S // LIST_ROWS)]
+        groups = [(0, halves[0]), (0, halves[1]), (1, slice(0, S)), (2, slice(0, S)), (3, slice(0, S))]
+        banks = [psum.tile([P, cols.stop - cols.start], F32, name="h_bank%d" % i, tag="bank%d" % i) for i, (t, cols) in enumerate(groups)]
+        for g in range(PASSES):
+            w1_codes, w1_plane = [], []
+            for u, engine_copy in enumerate((nc.vector.tensor_copy, nc.scalar.copy)):
+                grouped = sb("w1_grouped%d_%d" % (g, u), [P, 2 * P * PACK], BF16)
+                engine_copy(
+                    out=grouped[:].rearrange("p (t m j) -> p m j t", t=2, j=PACK),
+                    in_=w1_raw[g][:].rearrange("p j (m t) -> p m j t", t=PACK)[:, :, :, 2 * u : 2 * u + 2],
+                )
+                codes = sb("w1_codes%d_%d" % (g, u), [P, 2 * P], U32)
+                plane = sb("w1_plane%d_%d" % (g, u), [P, 2 * P], U8)
+                nc.vector.quantize_mx(out=codes[:].bitcast(FP8X4), scales=plane[:], in_=grouped[:])
+                w1_codes.append(codes)
+                w1_plane.append(plane)
+            x_codes = sb("x_codes%d" % g, [P, S], U32)
+            if g == 0:
+                nc.vector.tensor_copy(x_codes[:], x_table[g][:].bitcast(U32).indirect(offs_sb[:]))
+            else:
+                for cols, list_cols in zip(halves, list_halves):
+                    nc.vector.tensor_copy(x_codes[:, cols], x_table[g][:].bitcast(U32).indirect(offs_sb[:, list_cols]))
+            for bank, (t, cols) in zip(banks, groups):
+                w_cols = slice((t % 2) * P, (t % 2 + 1) * P)
+                nc.tensor.matmul_mx(
+                    out=bank[:],
+                    lhsT=w1_codes[t // 2][:, w_cols].bitcast(FP8X4),
+                    lhsT_scale=w1_plane[t // 2][:, w_cols],
+                    rhs=x_codes[:, cols].bitcast(FP8X4),
+                    rhs_scale=x_plane[4 * g : P, cols],
+                    start=(g == 0),
+                    stop=(g == PASSES - 1),
+                )
+
+        z_pair = [[sb("z%d_%d" % (u, a), [P, 2, b - a], F32) for a, b in CELL_PIECES] for u in range(2)]
+        z_grouped = [sb("z_grouped%d" % a, [P, (b - a) * PACK], BF16) for a, b in CELL_PIECES]
+
+        def add_skip(t):
+            for i, (a, b) in enumerate(CELL_PIECES):
+                nc.vector.tensor_tensor(z_pair[t // 2][i][:, t % 2, :], up[t][:, a:b], skip_sb[t][:, a:b], ADD)
+
+        def weave(engine_copy, u, i):
+            engine_copy(
+                out=z_grouped[i][:].rearrange("p (c e u t) -> p u c t e", e=4, u=2, t=2)[:, u],
+                in_=z_pair[u][i][:].rearrange("p t (c e) -> p c t e", e=4),
+            )
+
+        h_tags = ["h0", "h1", "skip0", "skip1"]
+        for t in range(PACK):
+            h = sb("h%d" % t, [P, S], F32, tag=h_tags[t])
+            for bank, (group_t, cols) in zip(banks, groups):
+                if group_t == t:
+                    nc.scalar.activation(h[:, cols], bank[:], GELU)
+                    list_cols = slice(cols.start // LIST_ROWS, cols.stop // LIST_ROWS)
+                    nc.vector.tensor_copy(up[t][:].indirect(cell_sb[:, list_cols]), h[:, cols])
+            add_skip(t)
+            if t == 1:
+                for i in range(len(CELL_PIECES)):
+                    weave(nc.scalar.copy, 0, i)
+
+        for i, (a, b) in enumerate(CELL_PIECES):
+            weave(nc.vector.tensor_copy if b - a == 512 else nc.scalar.copy, 1, i)
+        for i, (a, b) in enumerate(CELL_PIECES):
+            z_codes = sb("z_codes%d" % a, [P, b - a], U32)
+            z_plane = sb("z_plane%d" % a, [P, b - a], U8)
+            nc.vector.quantize_mx(out=z_codes[:].bitcast(FP8X4), scales=z_plane[:], in_=z_grouped[i][:])
+            acc = psum.tile([P, b - a], F32, name="out_bank%d" % i, tag="bank%d" % (5 + i))
+            nc.tensor.matmul_mx(
+                out=acc[:],
+                lhsT=w2_codes[:].bitcast(FP8X4),
+                lhsT_scale=w2_plane[:],
+                rhs=z_codes[:].bitcast(FP8X4),
+                rhs_scale=z_plane[:],
+                start=True,
+                stop=True,
+            )
+            result = sb("result%d" % a, [P, b - a], F32)
+            if i == len(CELL_PIECES) - 1:
+                nc.vector.tensor_copy(out=result[:], in_=acc[:])
+            else:
+                nc.scalar.copy(out=result[:], in_=acc[:])
+            nc.sync.dma_start(out=out[:, a:b], in_=result[:])

@@ -37,10 +37,10 @@ def tile_picked_unet_gelu_p_kernel(
         offs_sb = keep.tile([P, S // LIST_ROWS], U16, name="offs_sb")
         cell_sb = keep.tile([P, S // LIST_ROWS], U16, name="cell_sb")
 
+        x_scale_table = sb("x_scale_table", [P, T], U8)
+        nc.gpsimd.memset(x_scale_table[:].bitcast(I32), 0)
         warm = sb("warm", [P, 16], F32)
         nc.vector.memset(warm[:, 0:8], 0.0)
-        x_scale_table = sb("x_scale_table", [P, T], U8)
-        nc.vector.memset(x_scale_table[:].bitcast(I32), 0)
         nc.scalar.activation(warm[:, 8:16], warm[:, 0:8], GELU)
 
         nc.sync.dma_start(offs_sb[:], offs)
@@ -49,13 +49,14 @@ def tile_picked_unet_gelu_p_kernel(
             raw = sb("w1_raw%d" % g, [P, PACK, H], F32)
             nc.sync.dma_start(out=raw[:], in_=w1[g * K_PASS : (g + 1) * K_PASS, :].rearrange("(p j) c -> p j c", j=PACK))
             w1_raw.append(raw)
+            if g == 0:
+                for q in range(4):
+                    nc.sync.dma_start(
+                        out=x_scale_table[32 * q : 32 * q + 8, :].bitcast(I32), in_=x_scales[:, 4 * q : 4 * q + 4, :].bitcast(I32)
+                    )
             table = sb("x_table%d" % g, [P, T], I32)
             nc.sync.dma_start(out=table[:], in_=x_words[g].rearrange("p n t -> p (n t)").bitcast(I32))
             x_table.append(table)
-            for r in range(4):
-                nc.scalar.dma_start(
-                    out=x_scale_table[4 * g + r : P : 32, :].bitcast(I32), in_=x_scales[g, r:16:4, :].bitcast(I32)
-                )
         nc.sync.dma_start(cell_sb[:], cell)
         skip_rows = skip.rearrange("(p t) v -> t p v", t=PACK)
         skip_sb = []
@@ -73,7 +74,7 @@ def tile_picked_unet_gelu_p_kernel(
         up = []
         for t in range(PACK):
             window = sb("up%d" % t, [P, U], F32)
-            nc.vector.memset(window[:], 0.0)
+            nc.gpsimd.memset(window[:], 0.0)
             up.append(window)
 
         x_plane = sb("x_plane", [P, S], U8)
@@ -115,20 +116,25 @@ def tile_picked_unet_gelu_p_kernel(
                     stop=(g == PASSES - 1),
                 )
 
-        z_pair = [[sb("z%d_%d" % (u, a), [P, 2, b - a], F32) for a, b in CELL_PIECES] for u in range(2)]
+        z_low = sb("z_low", [P, 2, U], F32)
+        z_pair = [[z_low[:, :, a:b] for a, b in CELL_PIECES], [sb("z_high%d" % a, [P, 2, b - a], F32)[:] for a, b in CELL_PIECES]]
         z_grouped = [sb("z_grouped%d" % a, [P, (b - a) * PACK], BF16) for a, b in CELL_PIECES]
 
         def add_skip(t):
+            if t < 2:
+                nc.gpsimd.tensor_tensor(z_low[:, t, :], up[t][:], skip_sb[t][:], ADD)
+                return
+            engine = nc.gpsimd if t == 2 else nc.vector
             for i, (a, b) in enumerate(CELL_PIECES):
-                nc.vector.tensor_tensor(z_pair[t // 2][i][:, t % 2, :], up[t][:, a:b], skip_sb[t][:, a:b], ADD)
+                engine.tensor_tensor(z_pair[1][i][:, t % 2, :], up[t][:, a:b], skip_sb[t][:, a:b], ADD)
 
         def weave(engine_copy, u, i):
             engine_copy(
                 out=z_grouped[i][:].rearrange("p (c e u t) -> p u c t e", e=4, u=2, t=2)[:, u],
-                in_=z_pair[u][i][:].rearrange("p t (c e) -> p c t e", e=4),
+                in_=z_pair[u][i].rearrange("p t (c e) -> p c t e", e=4),
             )
 
-        h_tags = ["h0", "h1", "skip0", "skip1"]
+        h_tags = ["h0", "h1", "h2", "h3"]
         for t in range(PACK):
             h = sb("h%d" % t, [P, S], F32, tag=h_tags[t])
             for bank, (group_t, cols) in zip(banks, groups):

@@ -1,6 +1,7 @@
 from contextlib import ExitStack
 
 import concourse.mybir as mybir
+from concourse.masks import make_identity
 
 K, T, S, H, N, U = 1024, 2048, 512, 512, 128, 1024
 FLOPS = 2 * K * H * S + 2 * H * N * U
@@ -20,7 +21,11 @@ PACK = 4
 K_PASS = P * PACK
 PASSES = K // K_PASS
 LIST_ROWS = 16
-CELL_PIECES = [(0, 256), (512, 1024), (256, 512)]
+HALF_H = H // 2
+M_HALF = HALF_H // PACK
+BANK = 512
+PIECE = 256
+CELL_PIECES = [(a, a + PIECE) for a in range(0, U, PIECE)]
 
 
 def tile_picked_unet_gelu_p_kernel(
@@ -34,6 +39,9 @@ def tile_picked_unet_gelu_p_kernel(
         def sb(name, shape, dtype, tag=None):
             return keep.tile(shape, dtype, name=name, tag=tag or name, align_bytes=64)
 
+        def bank(name, number, width):
+            return psum.tile([P, width], F32, name=name, tag="bank%d" % number)
+
         offs_sb = keep.tile([P, S // LIST_ROWS], U16, name="offs_sb")
         cell_sb = keep.tile([P, S // LIST_ROWS], U16, name="cell_sb")
 
@@ -43,26 +51,35 @@ def tile_picked_unet_gelu_p_kernel(
         nc.vector.memset(warm[:, 0:8], 0.0)
         nc.scalar.activation(warm[:, 8:16], warm[:, 0:8], GELU)
 
-        nc.sync.dma_start(offs_sb[:], offs)
-        w1_raw, x_table = [], []
-        for g in range(PASSES):
-            raw = sb("w1_raw%d" % g, [P, PACK, H], F32)
-            nc.sync.dma_start(out=raw[:], in_=w1[g * K_PASS : (g + 1) * K_PASS, :].rearrange("(p j) c -> p j c", j=PACK))
-            w1_raw.append(raw)
-            if g == 0:
-                for q in range(4):
-                    nc.sync.dma_start(
-                        out=x_scale_table[32 * q : 32 * q + 8, :].bitcast(I32), in_=x_scales[:, 4 * q : 4 * q + 4, :].bitcast(I32)
-                    )
+        def load_x(g):
             table = sb("x_table%d" % g, [P, T], I32)
             nc.sync.dma_start(out=table[:], in_=x_words[g].rearrange("p n t -> p (n t)").bitcast(I32))
-            x_table.append(table)
+            return table
+
+        def load_w1(side, g):
+            raw = sb("w1_raw%d_%d" % (side, g), [P, PACK, HALF_H], F32)
+            rows = w1[g * K_PASS : (g + 1) * K_PASS, side * HALF_H : (side + 1) * HALF_H]
+            nc.sync.dma_start(out=raw[:], in_=rows.rearrange("(p j) c -> p j c", j=PACK))
+            return raw
+
+        nc.sync.dma_start(offs_sb[:], offs)
+        x_table = [load_x(0)]
+        for q in range(4):
+            nc.sync.dma_start(
+                out=x_scale_table[32 * q : 32 * q + 8, :].bitcast(I32), in_=x_scales[:, 4 * q : 4 * q + 4, :].bitcast(I32)
+            )
+        w1_raw = [[load_w1(0, g) for g in range(PASSES)]]
+        x_table.append(load_x(1))
         nc.sync.dma_start(cell_sb[:], cell)
-        skip_rows = skip.rearrange("(p t) v -> t p v", t=PACK)
+        w1_raw.append([load_w1(1, g) for g in range(PASSES)])
+        skip_by_slot = skip.rearrange("(m t) v -> m t v", t=PACK)
         skip_sb = []
-        for t in range(PACK):
-            plane = sb("skip%d" % t, [P, U], F32)
-            nc.sync.dma_start(out=plane[:], in_=skip_rows[t])
+        for s in range(PACK):
+            plane = sb("skip%d" % s, [P, U], F32)
+            if s < 2:
+                nc.sync.dma_start(out=plane[:], in_=skip_by_slot[s * M_HALF : (s + 1) * M_HALF, 0:2, :])
+            else:
+                nc.sync.dma_start(out=plane[:], in_=skip_by_slot[:, s, :])
             skip_sb.append(plane)
         w2_codes = sb("w2_codes", [P, N], I32)
         nc.sync.dma_start(out=w2_codes[:], in_=w2_words[0].rearrange("p n t -> p (n t)").bitcast(I32))
@@ -72,88 +89,151 @@ def tile_picked_unet_gelu_p_kernel(
             nc.sync.dma_start(out=w2_plane[r:P:32, :].bitcast(I32), in_=w2_scales[0, r:16:4, :].bitcast(I32))
 
         up = []
-        for t in range(PACK):
-            window = sb("up%d" % t, [P, U], F32)
+        for s in range(PACK):
+            window = sb("up%d" % s, [P, U], F32)
             nc.gpsimd.memset(window[:], 0.0)
             up.append(window)
-
-        x_plane = sb("x_plane", [P, S], U8)
-        nc.vector.tensor_copy(x_plane[:], x_scale_table[:].indirect(offs_sb[:]))
+        ident = sb("ident", [P, P], F32)
+        make_identity(nc, ident[:])
 
         half = S // 2
         halves = [slice(0, half), slice(half, S)]
         list_halves = [slice(0, half // LIST_ROWS), slice(half // LIST_ROWS, S // LIST_ROWS)]
-        groups = [(0, halves[0]), (0, halves[1]), (1, slice(0, S)), (2, slice(0, S)), (3, slice(0, S))]
-        banks = [psum.tile([P, cols.stop - cols.start], F32, name="h_bank%d" % i, tag="bank%d" % i) for i, (t, cols) in enumerate(groups)]
-        for g in range(PASSES):
-            w1_codes, w1_plane = [], []
-            for u, engine_copy in enumerate((nc.vector.tensor_copy, nc.scalar.copy)):
-                grouped = sb("w1_grouped%d_%d" % (g, u), [P, 2 * P * PACK], BF16)
-                engine_copy(
-                    out=grouped[:].rearrange("p (t m j) -> p m j t", t=2, j=PACK),
-                    in_=w1_raw[g][:].rearrange("p j (m t) -> p m j t", t=PACK)[:, :, :, 2 * u : 2 * u + 2],
-                )
-                codes = sb("w1_codes%d_%d" % (g, u), [P, 2 * P], U32)
-                plane = sb("w1_plane%d_%d" % (g, u), [P, 2 * P], U8)
-                nc.vector.quantize_mx(out=codes[:].bitcast(FP8X4), scales=plane[:], in_=grouped[:])
-                w1_codes.append(codes)
-                w1_plane.append(plane)
-            x_codes = sb("x_codes%d" % g, [P, S], U32)
-            if g == 0:
-                nc.vector.tensor_copy(x_codes[:], x_table[g][:].bitcast(U32).indirect(offs_sb[:]))
-            else:
-                for cols, list_cols in zip(halves, list_halves):
-                    nc.vector.tensor_copy(x_codes[:, cols], x_table[g][:].bitcast(U32).indirect(offs_sb[:, list_cols]))
-            for bank, (t, cols) in zip(banks, groups):
-                w_cols = slice((t % 2) * P, (t % 2 + 1) * P)
-                nc.tensor.matmul_mx(
-                    out=bank[:],
-                    lhsT=w1_codes[t // 2][:, w_cols].bitcast(FP8X4),
-                    lhsT_scale=w1_plane[t // 2][:, w_cols],
-                    rhs=x_codes[:, cols].bitcast(FP8X4),
-                    rhs_scale=x_plane[4 * g : P, cols],
-                    start=(g == 0),
-                    stop=(g == PASSES - 1),
-                )
 
-        z_low = sb("z_low", [P, 2, U], F32)
-        z_pair = [[z_low[:, :, a:b] for a, b in CELL_PIECES], [sb("z_high%d" % a, [P, 2, b - a], F32)[:] for a, b in CELL_PIECES]]
-        z_grouped = [sb("z_grouped%d" % a, [P, (b - a) * PACK], BF16) for a, b in CELL_PIECES]
+        x_codes = [sb("x_codes%d" % g, [P, S], U32) for g in range(PASSES)]
+        x_plane = sb("x_plane", [P, S], U8)
+        nc.vector.tensor_copy(x_codes[0][:], x_table[0][:].bitcast(U32).indirect(offs_sb[:]))
+        nc.vector.tensor_copy(x_plane[:], x_scale_table[:].indirect(offs_sb[:]))
 
-        def add_skip(t):
-            if t < 2:
-                nc.gpsimd.tensor_tensor(z_low[:, t, :], up[t][:], skip_sb[t][:], ADD)
-                return
-            engine = nc.gpsimd if t == 2 else nc.vector
-            for i, (a, b) in enumerate(CELL_PIECES):
-                engine.tensor_tensor(z_pair[1][i][:, t % 2, :], up[t][:, a:b], skip_sb[t][:, a:b], ADD)
+        low_in = [[sb("low_in%d_%d" % (side, g), [P, P * PACK], BF16) for g in range(PASSES)] for side in range(2)]
+        high_in = [sb("high_in%d" % g, [P, 2 * P * PACK], BF16) for g in range(PASSES)]
+        codes, planes = {}, {}
 
-        def weave(engine_copy, u, i):
+        def cast_low(engine_copy, side, g):
             engine_copy(
-                out=z_grouped[i][:].rearrange("p (c e u t) -> p u c t e", e=4, u=2, t=2)[:, u],
-                in_=z_pair[u][i].rearrange("p t (c e) -> p c t e", e=4),
+                out=low_in[side][g][:].rearrange("p (m e j) -> p m j e", e=2, j=PACK),
+                in_=w1_raw[side][g][:].rearrange("p j (m t) -> p m j t", t=PACK)[:, :, :, 0:2],
             )
 
-        h_tags = ["h0", "h1", "h2", "h3"]
-        for t in range(PACK):
-            h = sb("h%d" % t, [P, S], F32, tag=h_tags[t])
-            for bank, (group_t, cols) in zip(banks, groups):
-                if group_t == t:
-                    nc.scalar.activation(h[:, cols], bank[:], GELU)
-                    list_cols = slice(cols.start // LIST_ROWS, cols.stop // LIST_ROWS)
-                    nc.vector.tensor_copy(up[t][:].indirect(cell_sb[:, list_cols]), h[:, cols])
-            add_skip(t)
-            if t == 1:
-                for i in range(len(CELL_PIECES)):
-                    weave(nc.scalar.copy, 0, i)
+        def cast_high(engine_copy, side, g):
+            engine_copy(
+                out=high_in[g][:].rearrange("p (e a m j) -> p a m j e", e=2, a=2, j=PACK)[:, side],
+                in_=w1_raw[side][g][:].rearrange("p j (m t) -> p m j t", t=PACK)[:, :, :, 2:4],
+            )
 
-        for i, (a, b) in enumerate(CELL_PIECES):
-            weave(nc.vector.tensor_copy if b - a == 512 else nc.scalar.copy, 1, i)
-        for i, (a, b) in enumerate(CELL_PIECES):
-            z_codes = sb("z_codes%d" % a, [P, b - a], U32)
-            z_plane = sb("z_plane%d" % a, [P, b - a], U8)
-            nc.vector.quantize_mx(out=z_codes[:].bitcast(FP8X4), scales=z_plane[:], in_=z_grouped[i][:])
-            acc = psum.tile([P, b - a], F32, name="out_bank%d" % i, tag="bank%d" % (5 + i))
+        def quantize(name, source, width):
+            c = sb(name + "_codes", [P, width], U32)
+            pl = sb(name + "_plane", [P, width], U8)
+            nc.vector.quantize_mx(out=c[:].bitcast(FP8X4), scales=pl[:], in_=source[:])
+            return c, pl
+
+        def quantize_low(side, g):
+            c, pl = quantize("low%d_%d" % (side, g), low_in[side][g], P)
+            codes[side, g], planes[side, g] = c[:], pl[:]
+
+        def quantize_high(g):
+            c, pl = quantize("high%d" % g, high_in[g], 2 * P)
+            for e in range(2):
+                codes[2 + e, g], planes[2 + e, g] = c[:, e * P : (e + 1) * P], pl[:, e * P : (e + 1) * P]
+
+        def first_product(acc, s, g, cols):
+            nc.tensor.matmul_mx(
+                out=acc[:],
+                lhsT=codes[s, g].bitcast(FP8X4),
+                lhsT_scale=planes[s, g],
+                rhs=x_codes[g][:, cols].bitcast(FP8X4),
+                rhs_scale=x_plane[4 * g : P, cols],
+                start=(g == 0),
+                stop=(g == PASSES - 1),
+            )
+
+        for g in range(PASSES):
+            cast_low(nc.vector.tensor_copy, 0, g)
+            cast_high(nc.scalar.copy, 0, g)
+            quantize_low(0, g)
+        first_banks = [bank("h0_bank%d" % i, i, half) for i in range(2)]
+        for i in range(2):
+            first_product(first_banks[i], 0, 0, halves[i])
+        for i in range(2):
+            nc.vector.tensor_copy(x_codes[1][:, halves[i]], x_table[1][:].bitcast(U32).indirect(offs_sb[:, list_halves[i]]))
+            first_product(first_banks[i], 0, 1, halves[i])
+
+        h0a = sb("h0a", [P, half], F32)
+        nc.scalar.activation(h0a[:], first_banks[0][:], GELU)
+        nc.vector.tensor_copy(up[0][:].indirect(cell_sb[:, list_halves[0]]), h0a[:])
+
+        for g in range(PASSES):
+            cast_low(nc.scalar.copy, 1, g)
+            cast_high(nc.scalar.copy, 1, g)
+        h_banks = {1: bank("h1_bank", 2, S)}
+        for g in range(PASSES):
+            quantize_low(1, g)
+            first_product(h_banks[1], 1, g, slice(0, S))
+        for g in range(PASSES):
+            quantize_high(g)
+
+        h0b = sb("h0b", [P, half], F32, tag="w1_raw1_1")
+        nc.scalar.activation(h0b[:], first_banks[1][:], GELU)
+        nc.vector.tensor_copy(up[0][:].indirect(cell_sb[:, list_halves[1]]), h0b[:])
+        h = {}
+        for s in range(1, PACK):
+            if s > 1:
+                h_banks[s] = bank("h%d_bank" % s, s - 1, S)
+                for g in range(PASSES):
+                    first_product(h_banks[s], s, g, slice(0, S))
+            h[s] = sb("h%d" % s, [P, S], F32)
+            nc.scalar.activation(h[s][:], h_banks[s][:], GELU)
+        for s in range(1, PACK):
+            nc.vector.tensor_copy(up[s][:].indirect(cell_sb[:]), h[s][:])
+
+        blocks = BANK // P
+        z_turned = [sb("z_turned%d" % i, [P, blocks, 2, P], BF16) for i in range(U // BANK)]
+        for s in range(2):
+            sums = [bank("sum%d_%d" % (s, i), ((0, 1), (2, 0))[s][i], BANK) for i in range(U // BANK)]
+            for source in (skip_sb[s], up[s]):
+                for i in range(U // BANK):
+                    for b in range(blocks):
+                        cells = slice(i * BANK + b * P, i * BANK + (b + 1) * P)
+                        nc.tensor.matmul(
+                            sums[i][:, b * P : (b + 1) * P],
+                            lhsT=source[:, cells],
+                            rhs=ident[:],
+                            is_transpose=True,
+                            start=(source is skip_sb[s] and b == 0),
+                            stop=(source is up[s] and b == blocks - 1),
+                        )
+            for i in range(U // BANK):
+                nc.scalar.copy(out=z_turned[i][:, :, s, :], in_=sums[i][:].rearrange("p (b q) -> p b q", q=P))
+
+        z_grouped = [sb("z_grouped%d" % a, [P, (b - a) * PACK], BF16) for a, b in CELL_PIECES]
+        for i in range(U // BANK):
+            back = bank("back%d" % i, 3 + i, BANK)
+            for b in range(blocks):
+                words = z_turned[i][:, b].rearrange("p s q -> p (s q)").bitcast(F32)
+                nc.tensor.transpose(back[:, b * P : (b + 1) * P], words, ident[:])
+            for (a, b), piece in zip(CELL_PIECES, z_grouped):
+                if a // BANK == i:
+                    nc.scalar.copy(
+                        out=piece[:].bitcast(F32).rearrange("p (c u) -> p u c", u=2)[:, 0],
+                        in_=back[:, a - i * BANK : b - i * BANK],
+                    )
+
+        z_high = sb("z_high", [P, 2, U], BF16, tag="z_turned1")
+        nc.gpsimd.tensor_tensor(z_high[:, 0, :], up[2][:], skip_sb[2][:], ADD)
+        for a, b in CELL_PIECES:
+            nc.vector.tensor_tensor(z_high[:, 1, a:b], up[3][:, a:b], skip_sb[3][:, a:b], ADD)
+
+        def weave(engine_copy, i):
+            a, b = CELL_PIECES[i]
+            engine_copy(
+                out=z_grouped[i][:].rearrange("p (c e u t) -> p u c t e", e=4, u=2, t=2)[:, 1],
+                in_=z_high[:, :, a:b].rearrange("p t (c e) -> p c t e", e=4),
+            )
+
+        def second_product(i, engine_copy):
+            a, b = CELL_PIECES[i]
+            z_codes, z_plane = quantize("z%d" % a, z_grouped[i], b - a)
+            acc = bank("out_bank%d" % i, (5, 6, 7, 1)[i], b - a)
             nc.tensor.matmul_mx(
                 out=acc[:],
                 lhsT=w2_codes[:].bitcast(FP8X4),
@@ -164,8 +244,14 @@ def tile_picked_unet_gelu_p_kernel(
                 stop=True,
             )
             result = sb("result%d" % a, [P, b - a], F32)
-            if i == len(CELL_PIECES) - 1:
-                nc.vector.tensor_copy(out=result[:], in_=acc[:])
-            else:
-                nc.scalar.copy(out=result[:], in_=acc[:])
+            engine_copy(out=result[:], in_=acc[:])
             nc.sync.dma_start(out=out[:, a:b], in_=result[:])
+
+        weave(nc.scalar.copy, 0)
+        weave(nc.scalar.copy, 1)
+        second_product(0, nc.scalar.copy)
+        weave(nc.vector.tensor_copy, 2)
+        weave(nc.vector.tensor_copy, 3)
+        second_product(1, nc.scalar.copy)
+        second_product(2, nc.scalar.copy)
+        second_product(3, nc.vector.tensor_copy)

@@ -24,8 +24,10 @@ LIST_ROWS = 16
 HALF_H = H // 2
 M_HALF = HALF_H // PACK
 BANK = 512
-PIECE = 256
-CELL_PIECES = [(a, a + PIECE) for a in range(0, U, PIECE)]
+SCALAR_PIECES = [(0, 256), (256, 512), (512, 640)]
+VECTOR_CELLS = (640, U)
+WOVEN_PIECES = SCALAR_PIECES + [VECTOR_CELLS]
+PRODUCT_PIECES = [(0, 256), (256, 512), (640, 896), (896, U), (512, 640)]
 
 
 def tile_picked_unet_gelu_p_kernel(
@@ -91,7 +93,7 @@ def tile_picked_unet_gelu_p_kernel(
         up = []
         for s in range(PACK):
             window = sb("up%d" % s, [P, U], F32)
-            nc.gpsimd.memset(window[:], 0.0)
+            (nc.vector if s < 2 else nc.gpsimd).memset(window[:], 0.0)
             up.append(window)
         ident = sb("ident", [P, P], F32)
         make_identity(nc, ident[:])
@@ -124,15 +126,15 @@ def tile_picked_unet_gelu_p_kernel(
         def quantize(name, source, width):
             c = sb(name + "_codes", [P, width], U32)
             pl = sb(name + "_plane", [P, width], U8)
-            nc.vector.quantize_mx(out=c[:].bitcast(FP8X4), scales=pl[:], in_=source[:])
+            nc.vector.quantize_mx(out=c[:].bitcast(FP8X4), scales=pl[:], in_=source)
             return c, pl
 
         def quantize_low(side, g):
-            c, pl = quantize("low%d_%d" % (side, g), low_in[side][g], P)
+            c, pl = quantize("low%d_%d" % (side, g), low_in[side][g][:], P)
             codes[side, g], planes[side, g] = c[:], pl[:]
 
         def quantize_high(g):
-            c, pl = quantize("high%d" % g, high_in[g], 2 * P)
+            c, pl = quantize("high%d" % g, high_in[g][:], 2 * P)
             for e in range(2):
                 codes[2 + e, g], planes[2 + e, g] = c[:, e * P : (e + 1) * P], pl[:, e * P : (e + 1) * P]
 
@@ -151,16 +153,21 @@ def tile_picked_unet_gelu_p_kernel(
             cast_low(nc.vector.tensor_copy, 0, g)
             cast_high(nc.scalar.copy, 0, g)
             quantize_low(0, g)
-        first_banks = [bank("h0_bank%d" % i, i, half) for i in range(2)]
-        for i in range(2):
-            first_product(first_banks[i], 0, 0, halves[i])
+        quarter = S // 4
+        parts = [slice(0, quarter), slice(quarter, half), halves[1]]
+        first_banks = [bank("h0_bank%d" % i, (5, 0, 1)[i], cols.stop - cols.start) for i, cols in enumerate(parts)]
+        for acc, cols in zip(first_banks, parts):
+            first_product(acc, 0, 0, cols)
         for i in range(2):
             nc.vector.tensor_copy(x_codes[1][:, halves[i]], x_table[1][:].bitcast(U32).indirect(offs_sb[:, list_halves[i]]))
-            first_product(first_banks[i], 0, 1, halves[i])
+        for acc, cols in zip(first_banks, parts):
+            first_product(acc, 0, 1, cols)
 
-        h0a = sb("h0a", [P, half], F32)
-        nc.scalar.activation(h0a[:], first_banks[0][:], GELU)
-        nc.vector.tensor_copy(up[0][:].indirect(cell_sb[:, list_halves[0]]), h0a[:])
+        for i in range(2):
+            h0a = sb("h0a%d" % i, [P, quarter], F32)
+            nc.scalar.activation(h0a[:], first_banks[i][:], GELU)
+            list_cols = slice(parts[i].start // LIST_ROWS, parts[i].stop // LIST_ROWS)
+            nc.vector.tensor_copy(up[0][:].indirect(cell_sb[:, list_cols]), h0a[:])
 
         for g in range(PASSES):
             cast_low(nc.scalar.copy, 1, g)
@@ -173,7 +180,7 @@ def tile_picked_unet_gelu_p_kernel(
             quantize_high(g)
 
         h0b = sb("h0b", [P, half], F32, tag="w1_raw1_1")
-        nc.scalar.activation(h0b[:], first_banks[1][:], GELU)
+        nc.scalar.activation(h0b[:], first_banks[2][:], GELU)
         nc.vector.tensor_copy(up[0][:].indirect(cell_sb[:, list_halves[1]]), h0b[:])
         h = {}
         for s in range(1, PACK):
@@ -205,35 +212,36 @@ def tile_picked_unet_gelu_p_kernel(
             for i in range(U // BANK):
                 nc.scalar.copy(out=z_turned[i][:, :, s, :], in_=sums[i][:].rearrange("p (b q) -> p b q", q=P))
 
-        z_grouped = [sb("z_grouped%d" % a, [P, (b - a) * PACK], BF16) for a, b in CELL_PIECES]
+        z_grouped = {a: sb("z_grouped%d" % a, [P, (b - a) * PACK], BF16) for a, b in WOVEN_PIECES}
         for i in range(U // BANK):
             back = bank("back%d" % i, 3 + i, BANK)
             for b in range(blocks):
                 words = z_turned[i][:, b].rearrange("p s q -> p (s q)").bitcast(F32)
                 nc.tensor.transpose(back[:, b * P : (b + 1) * P], words, ident[:])
-            for (a, b), piece in zip(CELL_PIECES, z_grouped):
+            for a, b in WOVEN_PIECES:
                 if a // BANK == i:
                     nc.scalar.copy(
-                        out=piece[:].bitcast(F32).rearrange("p (c u) -> p u c", u=2)[:, 0],
-                        in_=back[:, a - i * BANK : b - i * BANK],
+                        out=z_grouped[a][:].bitcast(F32).rearrange("p (c u) -> p c u", u=2),
+                        in_=back[:, a - i * BANK : b - i * BANK].unsqueeze(2).to_broadcast([P, b - a, 2]),
                     )
 
         z_high = sb("z_high", [P, 2, U], BF16, tag="z_turned1")
         nc.gpsimd.tensor_tensor(z_high[:, 0, :], up[2][:], skip_sb[2][:], ADD)
-        for a, b in CELL_PIECES:
+        for a, b in [(0, 256), (256, 640), VECTOR_CELLS]:
             nc.vector.tensor_tensor(z_high[:, 1, a:b], up[3][:, a:b], skip_sb[3][:, a:b], ADD)
 
-        def weave(engine_copy, i):
-            a, b = CELL_PIECES[i]
+        def weave(engine_copy, a, b):
             engine_copy(
-                out=z_grouped[i][:].rearrange("p (c e u t) -> p u c t e", e=4, u=2, t=2)[:, 1],
+                out=z_grouped[a][:].rearrange("p (c e u t) -> p u c t e", e=4, u=2, t=2)[:, 1],
                 in_=z_high[:, :, a:b].rearrange("p t (c e) -> p c t e", e=4),
             )
 
         def second_product(i, engine_copy):
-            a, b = CELL_PIECES[i]
-            z_codes, z_plane = quantize("z%d" % a, z_grouped[i], b - a)
-            acc = bank("out_bank%d" % i, (5, 6, 7, 1)[i], b - a)
+            a, b = PRODUCT_PIECES[i]
+            start = max(first for first, last in WOVEN_PIECES if first <= a)
+            source = z_grouped[start][:, (a - start) * PACK : (b - start) * PACK]
+            z_codes, z_plane = quantize("z%d" % a, source, b - a)
+            acc = bank("out_bank%d" % i, (5, 6, 7, 1, 2)[i], b - a)
             nc.tensor.matmul_mx(
                 out=acc[:],
                 lhsT=w2_codes[:].bitcast(FP8X4),
@@ -247,11 +255,11 @@ def tile_picked_unet_gelu_p_kernel(
             engine_copy(out=result[:], in_=acc[:])
             nc.sync.dma_start(out=out[:, a:b], in_=result[:])
 
-        weave(nc.scalar.copy, 0)
-        weave(nc.scalar.copy, 1)
+        for a, b in SCALAR_PIECES:
+            weave(nc.scalar.copy, a, b)
         second_product(0, nc.scalar.copy)
-        weave(nc.vector.tensor_copy, 2)
-        weave(nc.vector.tensor_copy, 3)
+        weave(nc.vector.tensor_copy, *VECTOR_CELLS)
         second_product(1, nc.scalar.copy)
         second_product(2, nc.scalar.copy)
-        second_product(3, nc.vector.tensor_copy)
+        second_product(3, nc.scalar.copy)
+        second_product(4, nc.vector.tensor_copy)

@@ -49,9 +49,6 @@ def tile_picked_unet_gelu_p_kernel(
 
         x_scale_table = sb("x_scale_table", [P, T], U8)
         nc.gpsimd.memset(x_scale_table[:].bitcast(I32), 0)
-        warm = sb("warm", [P, 16], F32)
-        nc.vector.memset(warm[:, 0:8], 0.0)
-        nc.scalar.activation(warm[:, 8:16], warm[:, 0:8], GELU)
 
         def load_x(g):
             table = sb("x_table%d" % g, [P, T], I32)
@@ -64,13 +61,16 @@ def tile_picked_unet_gelu_p_kernel(
             nc.sync.dma_start(out=raw[:], in_=rows.rearrange("(p j) c -> p j c", j=PACK))
             return raw
 
-        nc.sync.dma_start(offs_sb[:], offs)
         x_table = [load_x(0)]
-        for q in range(4):
-            nc.sync.dma_start(
-                out=x_scale_table[32 * q : 32 * q + 8, :].bitcast(I32), in_=x_scales[:, 4 * q : 4 * q + 4, :].bitcast(I32)
-            )
+        nc.sync.dma_start(offs_sb[:], offs)
+
+        def load_x_scales(g):
+            for r in range(4):
+                nc.sync.dma_start(out=x_scale_table[4 * g + r : P : 32, :].bitcast(I32), in_=x_scales[g, r:16:4, :].bitcast(I32))
+
+        load_x_scales(0)
         w1_raw = [[load_w1(0, g) for g in range(PASSES)]]
+        load_x_scales(1)
         x_table.append(load_x(1))
         nc.sync.dma_start(cell_sb[:], cell)
         w1_raw.append([load_w1(1, g) for g in range(PASSES)])
@@ -90,11 +90,11 @@ def tile_picked_unet_gelu_p_kernel(
         for r in range(4):
             nc.sync.dma_start(out=w2_plane[r:P:32, :].bitcast(I32), in_=w2_scales[0, r:16:4, :].bitcast(I32))
 
-        up = []
-        for s in range(PACK):
-            window = sb("up%d" % s, [P, U], F32)
-            (nc.vector if s < 2 else nc.gpsimd).memset(window[:], 0.0)
-            up.append(window)
+        up = [sb("up%d" % s, [P, U], F32) for s in range(PACK)]
+        nc.vector.memset(up[1][:], 0.0)
+        nc.scalar.activation(up[0][:], up[1][:], GELU)
+        for s in range(2, PACK):
+            nc.gpsimd.memset(up[s][:], 0.0)
         ident = sb("ident", [P, P], F32)
         make_identity(nc, ident[:])
 
@@ -123,8 +123,8 @@ def tile_picked_unet_gelu_p_kernel(
                 in_=w1_raw[side][g][:].rearrange("p j (m t) -> p m j t", t=PACK)[:, :, :, 2:4],
             )
 
-        def quantize(name, source, width):
-            c = sb(name + "_codes", [P, width], U32)
+        def quantize(name, source, width, tag=None):
+            c = sb(name + "_codes", [P, width], U32, tag=tag)
             pl = sb(name + "_plane", [P, width], U8)
             nc.vector.quantize_mx(out=c[:].bitcast(FP8X4), scales=pl[:], in_=source)
             return c, pl
@@ -134,7 +134,7 @@ def tile_picked_unet_gelu_p_kernel(
             codes[side, g], planes[side, g] = c[:], pl[:]
 
         def quantize_high(g):
-            c, pl = quantize("high%d" % g, high_in[g][:], 2 * P)
+            c, pl = quantize("high%d" % g, high_in[g][:], 2 * P, tag="low_in1_%d" % (1 - g))
             for e in range(2):
                 codes[2 + e, g], planes[2 + e, g] = c[:, e * P : (e + 1) * P], pl[:, e * P : (e + 1) * P]
 

@@ -15,6 +15,7 @@ U8 = mybir.dt.uint8
 FP8X4 = mybir.dt.float8_e4m3fn_x4
 GELU = mybir.ActivationFunctionType.Gelu_apprx_tanh
 ADD = mybir.AluOpType.add
+MULT = mybir.AluOpType.mult
 
 P = 128
 PACK = 4
@@ -27,7 +28,7 @@ BANK = 512
 SCALAR_PIECES = [(0, 256), (256, 512), (512, 640)]
 VECTOR_CELLS = (640, U)
 WOVEN_PIECES = SCALAR_PIECES + [VECTOR_CELLS]
-PRODUCT_PIECES = [(0, 256), (256, 512), (640, 896), (896, U), (512, 640)]
+PRODUCT_PIECES = [(0, 256), (640, 896), (896, U), (256, 512), (512, 640)]
 
 
 def tile_picked_unet_gelu_p_kernel(
@@ -61,7 +62,7 @@ def tile_picked_unet_gelu_p_kernel(
             nc.sync.dma_start(out=raw[:], in_=rows.rearrange("(p j) c -> p j c", j=PACK))
             return raw
 
-        x_table = [load_x(0)]
+        w1_raw = [[load_w1(0, 0)]]
         nc.sync.dma_start(offs_sb[:], offs)
 
         def load_x_scales(g):
@@ -69,7 +70,8 @@ def tile_picked_unet_gelu_p_kernel(
                 nc.sync.dma_start(out=x_scale_table[4 * g + r : P : 32, :].bitcast(I32), in_=x_scales[g, r:16:4, :].bitcast(I32))
 
         load_x_scales(0)
-        w1_raw = [[load_w1(0, g) for g in range(PASSES)]]
+        x_table = [load_x(0)]
+        w1_raw[0].append(load_w1(0, 1))
         load_x_scales(1)
         x_table.append(load_x(1))
         nc.sync.dma_start(cell_sb[:], cell)
@@ -104,12 +106,17 @@ def tile_picked_unet_gelu_p_kernel(
 
         x_codes = [sb("x_codes%d" % g, [P, S], U32) for g in range(PASSES)]
         x_plane = sb("x_plane", [P, S], U8)
-        nc.vector.tensor_copy(x_codes[0][:], x_table[0][:].bitcast(U32).indirect(offs_sb[:]))
-        nc.vector.tensor_copy(x_plane[:], x_scale_table[:].indirect(offs_sb[:]))
 
         low_in = [[sb("low_in%d_%d" % (side, g), [P, P * PACK], BF16) for g in range(PASSES)] for side in range(2)]
         high_in = [sb("high_in%d" % g, [P, 2 * P * PACK], BF16) for g in range(PASSES)]
         codes, planes = {}, {}
+
+        def casts_on_gpsimd(side, g):
+            low = low_in[side][g][:].rearrange("p (m e j) -> p m e j", e=2, j=PACK)
+            high = high_in[g][:].rearrange("p (e a m j) -> p a e m j", e=2, a=2, j=PACK)[:, side]
+            raw = w1_raw[side][g][:]
+            nc.gpsimd.tensor_scalar(low, raw.rearrange("p j (m t) -> p m t j", t=PACK)[:, :, 0:2], 1.0, 0.0, MULT, ADD)
+            nc.gpsimd.tensor_scalar(high, raw.rearrange("p j (m t) -> p t m j", t=PACK)[:, 2:4], 1.0, 0.0, MULT, ADD)
 
         def cast_low(engine_copy, side, g):
             engine_copy(
@@ -129,8 +136,8 @@ def tile_picked_unet_gelu_p_kernel(
             nc.vector.quantize_mx(out=c[:].bitcast(FP8X4), scales=pl[:], in_=source)
             return c, pl
 
-        def quantize_low(side, g):
-            c, pl = quantize("low%d_%d" % (side, g), low_in[side][g][:], P)
+        def quantize_low(side, g, tag=None):
+            c, pl = quantize("low%d_%d" % (side, g), low_in[side][g][:], P, tag=tag)
             codes[side, g], planes[side, g] = c[:], pl[:]
 
         def quantize_high(g):
@@ -150,28 +157,26 @@ def tile_picked_unet_gelu_p_kernel(
             )
 
         for g in range(PASSES):
-            cast_low(nc.vector.tensor_copy, 0, g)
+            cast_low(nc.scalar.copy, 0, g)
             cast_high(nc.scalar.copy, 0, g)
-            quantize_low(0, g)
-        quarter = S // 4
-        parts = [slice(0, quarter), slice(quarter, half), halves[1]]
-        first_banks = [bank("h0_bank%d" % i, (5, 0, 1)[i], cols.stop - cols.start) for i, cols in enumerate(parts)]
-        for acc, cols in zip(first_banks, parts):
-            first_product(acc, 0, 0, cols)
+        quantize_low(0, 0)
+        nc.vector.tensor_copy(x_codes[0][:], x_table[0][:].bitcast(U32).indirect(offs_sb[:]))
+        nc.vector.tensor_copy(x_plane[:], x_scale_table[:].indirect(offs_sb[:]))
+        quantize_low(0, 1, tag="x_scale_table")
+        first_banks = [bank("h0_bank%d" % i, i, half) for i in range(2)]
+        for i in range(2):
+            first_product(first_banks[i], 0, 0, halves[i])
         for i in range(2):
             nc.vector.tensor_copy(x_codes[1][:, halves[i]], x_table[1][:].bitcast(U32).indirect(offs_sb[:, list_halves[i]]))
-        for acc, cols in zip(first_banks, parts):
-            first_product(acc, 0, 1, cols)
+            first_product(first_banks[i], 0, 1, halves[i])
 
-        for i in range(2):
-            h0a = sb("h0a%d" % i, [P, quarter], F32)
-            nc.scalar.activation(h0a[:], first_banks[i][:], GELU)
-            list_cols = slice(parts[i].start // LIST_ROWS, parts[i].stop // LIST_ROWS)
-            nc.vector.tensor_copy(up[0][:].indirect(cell_sb[:, list_cols]), h0a[:])
+        h0a = sb("h0a", [P, half], F32)
+        nc.scalar.activation(h0a[:], first_banks[0][:], GELU)
+        nc.vector.tensor_copy(up[0][:].indirect(cell_sb[:, list_halves[0]]), h0a[:])
 
-        for g in range(PASSES):
-            cast_low(nc.scalar.copy, 1, g)
-            cast_high(nc.scalar.copy, 1, g)
+        casts_on_gpsimd(1, 0)
+        cast_low(nc.scalar.copy, 1, 1)
+        cast_high(nc.scalar.copy, 1, 1)
         h_banks = {1: bank("h1_bank", 2, S)}
         for g in range(PASSES):
             quantize_low(1, g)
@@ -180,7 +185,7 @@ def tile_picked_unet_gelu_p_kernel(
             quantize_high(g)
 
         h0b = sb("h0b", [P, half], F32, tag="w1_raw1_1")
-        nc.scalar.activation(h0b[:], first_banks[2][:], GELU)
+        nc.scalar.activation(h0b[:], first_banks[1][:], GELU)
         nc.vector.tensor_copy(up[0][:].indirect(cell_sb[:, list_halves[1]]), h0b[:])
         h = {}
         for s in range(1, PACK):
@@ -225,9 +230,9 @@ def tile_picked_unet_gelu_p_kernel(
                         in_=back[:, a - i * BANK : b - i * BANK].unsqueeze(2).to_broadcast([P, b - a, 2]),
                     )
 
-        z_high = sb("z_high", [P, 2, U], BF16, tag="z_turned1")
+        z_high = sb("z_high", [P, 2, U], BF16, tag="z_turned0")
         nc.gpsimd.tensor_tensor(z_high[:, 0, :], up[2][:], skip_sb[2][:], ADD)
-        for a, b in [(0, 256), (256, 640), VECTOR_CELLS]:
+        for a, b in [(0, 256), VECTOR_CELLS, (256, 640)]:
             nc.vector.tensor_tensor(z_high[:, 1, a:b], up[3][:, a:b], skip_sb[3][:, a:b], ADD)
 
         def weave(engine_copy, a, b):
@@ -257,8 +262,8 @@ def tile_picked_unet_gelu_p_kernel(
 
         for a, b in SCALAR_PIECES:
             weave(nc.scalar.copy, a, b)
-        second_product(0, nc.scalar.copy)
         weave(nc.vector.tensor_copy, *VECTOR_CELLS)
+        second_product(0, nc.scalar.copy)
         second_product(1, nc.scalar.copy)
         second_product(2, nc.scalar.copy)
         second_product(3, nc.scalar.copy)

@@ -71,20 +71,20 @@ def tile_picked_unet_gelu_p_kernel(
 
         load_x_scales(0)
         x_table = [load_x(0)]
-        w1_raw[0].append(load_w1(0, 1))
         load_x_scales(1)
+        w1_raw[0].append(load_w1(0, 1))
         x_table.append(load_x(1))
         nc.sync.dma_start(cell_sb[:], cell)
         w1_raw.append([load_w1(1, g) for g in range(PASSES)])
         skip_by_slot = skip.rearrange("(m t) v -> m t v", t=PACK)
-        skip_sb = []
-        for s in range(PACK):
+        skip_sb = {}
+        for s in (2, 3, 0, 1):
             plane = sb("skip%d" % s, [P, U], F32)
             if s < 2:
                 nc.sync.dma_start(out=plane[:], in_=skip_by_slot[s * M_HALF : (s + 1) * M_HALF, 0:2, :])
             else:
                 nc.sync.dma_start(out=plane[:], in_=skip_by_slot[:, s, :])
-            skip_sb.append(plane)
+            skip_sb[s] = plane
         w2_codes = sb("w2_codes", [P, N], I32)
         nc.sync.dma_start(out=w2_codes[:], in_=w2_words[0].rearrange("p n t -> p (n t)").bitcast(I32))
         w2_plane = sb("w2_plane", [P, N], U8)
@@ -97,6 +97,8 @@ def tile_picked_unet_gelu_p_kernel(
         nc.scalar.activation(up[0][:], up[1][:], GELU)
         for s in range(2, PACK):
             nc.gpsimd.memset(up[s][:], 0.0)
+        up_second = sb("up_second", [P, U], F32)
+        nc.gpsimd.memset(up_second[:], 0.0)
         ident = sb("ident", [P, P], F32)
         make_identity(nc, ident[:])
 
@@ -111,11 +113,14 @@ def tile_picked_unet_gelu_p_kernel(
         high_in = [sb("high_in%d" % g, [P, 2 * P * PACK], BF16) for g in range(PASSES)]
         codes, planes = {}, {}
 
-        def casts_on_gpsimd(side, g):
+        def gpsimd_cast_low(side, g):
             low = low_in[side][g][:].rearrange("p (m e j) -> p m e j", e=2, j=PACK)
-            high = high_in[g][:].rearrange("p (e a m j) -> p a e m j", e=2, a=2, j=PACK)[:, side]
             raw = w1_raw[side][g][:]
             nc.gpsimd.tensor_scalar(low, raw.rearrange("p j (m t) -> p m t j", t=PACK)[:, :, 0:2], 1.0, 0.0, MULT, ADD)
+
+        def gpsimd_cast_high(side, g):
+            high = high_in[g][:].rearrange("p (e a m j) -> p a e m j", e=2, a=2, j=PACK)[:, side]
+            raw = w1_raw[side][g][:]
             nc.gpsimd.tensor_scalar(high, raw.rearrange("p j (m t) -> p t m j", t=PACK)[:, 2:4], 1.0, 0.0, MULT, ADD)
 
         def cast_low(engine_copy, side, g):
@@ -140,10 +145,21 @@ def tile_picked_unet_gelu_p_kernel(
             c, pl = quantize("low%d_%d" % (side, g), low_in[side][g][:], P, tag=tag)
             codes[side, g], planes[side, g] = c[:], pl[:]
 
-        def quantize_high(g):
-            c, pl = quantize("high%d" % g, high_in[g][:], 2 * P, tag="low_in1_%d" % (1 - g))
+        high_codes = [sb("high_codes%d" % g, [P, 2 * P], U32) for g in range(PASSES)]
+        high_plane = [sb("high_plane%d" % g, [P, 2 * P], U8) for g in range(PASSES)]
+        for g in range(PASSES):
             for e in range(2):
-                codes[2 + e, g], planes[2 + e, g] = c[:, e * P : (e + 1) * P], pl[:, e * P : (e + 1) * P]
+                codes[2 + e, g] = high_codes[g][:, e * P : (e + 1) * P]
+                planes[2 + e, g] = high_plane[g][:, e * P : (e + 1) * P]
+
+        def quantize_high(side, g):
+            for e in range(2):
+                first = e * P + side * M_HALF
+                nc.vector.quantize_mx(
+                    out=high_codes[g][:, first : first + M_HALF].bitcast(FP8X4),
+                    scales=high_plane[g][:, first : first + M_HALF],
+                    in_=high_in[g][:, first * PACK : (first + M_HALF) * PACK],
+                )
 
         def first_product(acc, s, g, cols):
             nc.tensor.matmul_mx(
@@ -162,39 +178,49 @@ def tile_picked_unet_gelu_p_kernel(
         quantize_low(0, 0)
         nc.vector.tensor_copy(x_codes[0][:], x_table[0][:].bitcast(U32).indirect(offs_sb[:]))
         nc.vector.tensor_copy(x_plane[:], x_scale_table[:].indirect(offs_sb[:]))
-        quantize_low(0, 1, tag="x_scale_table")
-        first_banks = [bank("h0_bank%d" % i, i, half) for i in range(2)]
-        for i in range(2):
-            first_product(first_banks[i], 0, 0, halves[i])
+        quantize_low(0, 1)
+        for g in range(PASSES):
+            quantize_high(0, g)
+        first_pieces = [(0, 128), (128, 256), (256, S)]
+        first_banks = [bank("h0_bank%d" % i, i, b - a) for i, (a, b) in enumerate(first_pieces)]
+        for i, (a, b) in enumerate(first_pieces):
+            first_product(first_banks[i], 0, 0, slice(a, b))
         for i in range(2):
             nc.vector.tensor_copy(x_codes[1][:, halves[i]], x_table[1][:].bitcast(U32).indirect(offs_sb[:, list_halves[i]]))
-            first_product(first_banks[i], 0, 1, halves[i])
+        for i, (a, b) in enumerate(first_pieces):
+            first_product(first_banks[i], 0, 1, slice(a, b))
 
-        h0a = sb("h0a", [P, half], F32)
-        nc.scalar.activation(h0a[:], first_banks[0][:], GELU)
-        nc.vector.tensor_copy(up[0][:].indirect(cell_sb[:, list_halves[0]]), h0a[:])
+        def first_scatter(i, tag=None):
+            a, b = first_pieces[i]
+            piece = sb("h0_%d" % i, [P, b - a], F32, tag=tag)
+            nc.scalar.activation(piece[:], first_banks[i][:], GELU)
+            window = up_second if i == 1 else up[0]
+            nc.vector.tensor_copy(window[:].indirect(cell_sb[:, a // LIST_ROWS : b // LIST_ROWS]), piece[:])
 
-        casts_on_gpsimd(1, 0)
+        first_scatter(0)
+        first_scatter(1)
+
+        gpsimd_cast_low(1, 0)
+        cast_high(nc.scalar.copy, 1, 0)
         cast_low(nc.scalar.copy, 1, 1)
-        cast_high(nc.scalar.copy, 1, 1)
-        h_banks = {1: bank("h1_bank", 2, S)}
+        gpsimd_cast_high(1, 1)
+        h1_banks = [bank("h1_bank%d" % i, 3 + i, half) for i in range(2)]
         for g in range(PASSES):
             quantize_low(1, g)
-            first_product(h_banks[1], 1, g, slice(0, S))
+            for i in range(2):
+                first_product(h1_banks[i], 1, g, halves[i])
         for g in range(PASSES):
-            quantize_high(g)
+            quantize_high(1, g)
 
-        h0b = sb("h0b", [P, half], F32, tag="w1_raw1_1")
-        nc.scalar.activation(h0b[:], first_banks[1][:], GELU)
-        nc.vector.tensor_copy(up[0][:].indirect(cell_sb[:, list_halves[1]]), h0b[:])
-        h = {}
-        for s in range(1, PACK):
-            if s > 1:
-                h_banks[s] = bank("h%d_bank" % s, s - 1, S)
-                for g in range(PASSES):
-                    first_product(h_banks[s], s, g, slice(0, S))
-            h[s] = sb("h%d" % s, [P, S], F32)
-            nc.scalar.activation(h[s][:], h_banks[s][:], GELU)
+        first_scatter(2, tag="w1_raw1_1")
+        h = {s: sb("h%d" % s, [P, S], F32) for s in range(1, PACK)}
+        for i in range(2):
+            nc.scalar.activation(h[1][:, halves[i]], h1_banks[i][:], GELU)
+        for s in range(2, PACK):
+            acc = bank("h%d_bank" % s, s + 1, S)
+            for g in range(PASSES):
+                first_product(acc, s, g, slice(0, S))
+            nc.scalar.activation(h[s][:], acc[:], GELU)
         for s in range(1, PACK):
             nc.vector.tensor_copy(up[s][:].indirect(cell_sb[:]), h[s][:])
 
@@ -202,7 +228,7 @@ def tile_picked_unet_gelu_p_kernel(
         z_turned = [sb("z_turned%d" % i, [P, blocks, 2, P], BF16) for i in range(U // BANK)]
         for s in range(2):
             sums = [bank("sum%d_%d" % (s, i), ((0, 1), (2, 0))[s][i], BANK) for i in range(U // BANK)]
-            for source in (skip_sb[s], up[s]):
+            for source in [skip_sb[s]] + [up_second] * (s == 0) + [up[s]]:
                 for i in range(U // BANK):
                     for b in range(blocks):
                         cells = slice(i * BANK + b * P, i * BANK + (b + 1) * P)

@@ -78,7 +78,7 @@ def tile_picked_unet_gelu_p_kernel(
         w1_raw.append([load_w1(1, g) for g in range(PASSES)])
         skip_by_slot = skip.rearrange("(m t) v -> m t v", t=PACK)
         skip_sb = {}
-        for s in (2, 3, 0, 1):
+        for s in range(PACK):
             plane = sb("skip%d" % s, [P, U], F32)
             if s < 2:
                 nc.sync.dma_start(out=plane[:], in_=skip_by_slot[s * M_HALF : (s + 1) * M_HALF, 0:2, :])
@@ -97,8 +97,6 @@ def tile_picked_unet_gelu_p_kernel(
         nc.scalar.activation(up[0][:], up[1][:], GELU)
         for s in range(2, PACK):
             nc.gpsimd.memset(up[s][:], 0.0)
-        up_second = sb("up_second", [P, U], F32)
-        nc.gpsimd.memset(up_second[:], 0.0)
         ident = sb("ident", [P, P], F32)
         make_identity(nc, ident[:])
 
@@ -190,20 +188,16 @@ def tile_picked_unet_gelu_p_kernel(
         for i, (a, b) in enumerate(first_pieces):
             first_product(first_banks[i], 0, 1, slice(a, b))
 
-        def first_scatter(i, tag=None):
+        h0a = sb("h0a", [P, half], F32)
+        for i in range(2):
             a, b = first_pieces[i]
-            piece = sb("h0_%d" % i, [P, b - a], F32, tag=tag)
-            nc.scalar.activation(piece[:], first_banks[i][:], GELU)
-            window = up_second if i == 1 else up[0]
-            nc.vector.tensor_copy(window[:].indirect(cell_sb[:, a // LIST_ROWS : b // LIST_ROWS]), piece[:])
-
-        first_scatter(0)
-        first_scatter(1)
+            nc.scalar.activation(h0a[:, a:b], first_banks[i][:], GELU)
+        nc.vector.tensor_copy(up[0][:].indirect(cell_sb[:, list_halves[0]]), h0a[:])
 
         gpsimd_cast_low(1, 0)
-        cast_high(nc.scalar.copy, 1, 0)
+        gpsimd_cast_high(1, 0)
         cast_low(nc.scalar.copy, 1, 1)
-        gpsimd_cast_high(1, 1)
+        cast_high(nc.scalar.copy, 1, 1)
         h1_banks = [bank("h1_bank%d" % i, 3 + i, half) for i in range(2)]
         for g in range(PASSES):
             quantize_low(1, g)
@@ -212,7 +206,9 @@ def tile_picked_unet_gelu_p_kernel(
         for g in range(PASSES):
             quantize_high(1, g)
 
-        first_scatter(2, tag="w1_raw1_1")
+        h0b = sb("h0b", [P, half], F32, tag="w1_raw1_1")
+        nc.scalar.activation(h0b[:], first_banks[2][:], GELU)
+        nc.vector.tensor_copy(up[0][:].indirect(cell_sb[:, list_halves[1]]), h0b[:])
         h = {s: sb("h%d" % s, [P, S], F32) for s in range(1, PACK)}
         for i in range(2):
             nc.scalar.activation(h[1][:, halves[i]], h1_banks[i][:], GELU)
@@ -224,39 +220,40 @@ def tile_picked_unet_gelu_p_kernel(
         for s in range(1, PACK):
             nc.vector.tensor_copy(up[s][:].indirect(cell_sb[:]), h[s][:])
 
-        blocks = BANK // P
-        z_turned = [sb("z_turned%d" % i, [P, blocks, 2, P], BF16) for i in range(U // BANK)]
+        blocks = BANK // (2 * P)
+        z_turned = [sb("z_turned%d" % i, [P, blocks, 2, 2, P], BF16) for i in range(U // BANK)]
         for s in range(2):
-            sums = [bank("sum%d_%d" % (s, i), ((0, 1), (2, 0))[s][i], BANK) for i in range(U // BANK)]
-            for source in [skip_sb[s]] + [up_second] * (s == 0) + [up[s]]:
-                for i in range(U // BANK):
-                    for b in range(blocks):
-                        cells = slice(i * BANK + b * P, i * BANK + (b + 1) * P)
-                        nc.tensor.matmul(
-                            sums[i][:, b * P : (b + 1) * P],
-                            lhsT=source[:, cells],
-                            rhs=ident[:],
-                            is_transpose=True,
-                            start=(source is skip_sb[s] and b == 0),
-                            stop=(source is up[s] and b == blocks - 1),
-                        )
             for i in range(U // BANK):
-                nc.scalar.copy(out=z_turned[i][:, :, s, :], in_=sums[i][:].rearrange("p (b q) -> p b q", q=P))
+                cells = slice(i * BANK, (i + 1) * BANK)
+                z_low = sb("z_low%d_%d" % (s, i), [P, BANK], BF16)
+                nc.gpsimd.tensor_tensor(z_low[:], up[s][:, cells], skip_sb[s][:, cells], ADD)
+                turned = bank("turned%d_%d" % (s, i), i, blocks * P)
+                for b in range(blocks):
+                    nc.tensor.transpose(turned[:, b * P : (b + 1) * P], z_low[:].bitcast(F32)[:, b * P : (b + 1) * P], ident[:])
+                nc.scalar.copy(
+                    out=z_turned[i][:, :, :, s, :],
+                    in_=turned[:].bitcast(BF16).rearrange("p (b q c) -> p b c q", b=blocks, c=2),
+                )
 
         z_grouped = {a: sb("z_grouped%d" % a, [P, (b - a) * PACK], BF16) for a, b in WOVEN_PIECES}
         for i in range(U // BANK):
             back = bank("back%d" % i, 3 + i, BANK)
             for b in range(blocks):
-                words = z_turned[i][:, b].rearrange("p s q -> p (s q)").bitcast(F32)
-                nc.tensor.transpose(back[:, b * P : (b + 1) * P], words, ident[:])
+                for c in range(2):
+                    words = z_turned[i][:, b, c].rearrange("p s q -> p (s q)").bitcast(F32)
+                    nc.tensor.transpose(back[:, (2 * b + c) * P : (2 * b + c + 1) * P], words, ident[:])
+            by_cell = back[:].rearrange("p (b c j) -> p b j c", b=blocks, c=2)
             for a, b in WOVEN_PIECES:
-                if a // BANK == i:
-                    nc.scalar.copy(
-                        out=z_grouped[a][:].bitcast(F32).rearrange("p (c u) -> p c u", u=2),
-                        in_=back[:, a - i * BANK : b - i * BANK].unsqueeze(2).to_broadcast([P, b - a, 2]),
-                    )
+                for first in range(i * BANK, (i + 1) * BANK, 2 * P):
+                    lo, hi = max(a, first), min(b, first + 2 * P)
+                    if lo < hi:
+                        source = by_cell[:, (first - i * BANK) // (2 * P), (lo - first) // 2 : (hi - first) // 2]
+                        nc.scalar.copy(
+                            out=z_grouped[a][:].bitcast(F32)[:, 2 * (lo - a) : 2 * (hi - a)].rearrange("p (j c u) -> p j c u", c=2, u=2),
+                            in_=source.unsqueeze(3).to_broadcast([P, (hi - lo) // 2, 2, 2]),
+                        )
 
-        z_high = sb("z_high", [P, 2, U], BF16, tag="z_turned0")
+        z_high = sb("z_high", [P, 2, U], BF16)
         nc.gpsimd.tensor_tensor(z_high[:, 0, :], up[2][:], skip_sb[2][:], ADD)
         for a, b in [(0, 256), VECTOR_CELLS, (256, 640)]:
             nc.vector.tensor_tensor(z_high[:, 1, a:b], up[3][:, a:b], skip_sb[3][:, a:b], ADD)

@@ -15,7 +15,6 @@ U8 = mybir.dt.uint8
 FP8X4 = mybir.dt.float8_e4m3fn_x4
 GELU = mybir.ActivationFunctionType.Gelu_apprx_tanh
 ADD = mybir.AluOpType.add
-MULT = mybir.AluOpType.mult
 
 P = 128
 PACK = 4
@@ -111,16 +110,6 @@ def tile_picked_unet_gelu_p_kernel(
         high_in = [sb("high_in%d" % g, [P, 2 * P * PACK], BF16) for g in range(PASSES)]
         codes, planes = {}, {}
 
-        def gpsimd_cast_low(side, g):
-            low = low_in[side][g][:].rearrange("p (m e j) -> p m e j", e=2, j=PACK)
-            raw = w1_raw[side][g][:]
-            nc.gpsimd.tensor_scalar(low, raw.rearrange("p j (m t) -> p m t j", t=PACK)[:, :, 0:2], 1.0, 0.0, MULT, ADD)
-
-        def gpsimd_cast_high(side, g):
-            high = high_in[g][:].rearrange("p (e a m j) -> p a e m j", e=2, a=2, j=PACK)[:, side]
-            raw = w1_raw[side][g][:]
-            nc.gpsimd.tensor_scalar(high, raw.rearrange("p j (m t) -> p t m j", t=PACK)[:, 2:4], 1.0, 0.0, MULT, ADD)
-
         def cast_low(engine_copy, side, g):
             engine_copy(
                 out=low_in[side][g][:].rearrange("p (m e j) -> p m j e", e=2, j=PACK),
@@ -194,21 +183,21 @@ def tile_picked_unet_gelu_p_kernel(
             nc.scalar.activation(h0a[:, a:b], first_banks[i][:], GELU)
         nc.vector.tensor_copy(up[0][:].indirect(cell_sb[:, list_halves[0]]), h0a[:])
 
-        gpsimd_cast_low(1, 0)
-        gpsimd_cast_high(1, 0)
+        cast_low(nc.scalar.copy, 1, 0)
+        cast_high(nc.scalar.copy, 1, 0)
         cast_low(nc.scalar.copy, 1, 1)
-        cast_high(nc.scalar.copy, 1, 1)
         h1_banks = [bank("h1_bank%d" % i, 3 + i, half) for i in range(2)]
         for g in range(PASSES):
             quantize_low(1, g)
             for i in range(2):
                 first_product(h1_banks[i], 1, g, halves[i])
-        for g in range(PASSES):
-            quantize_high(1, g)
+        quantize_high(1, 0)
 
-        h0b = sb("h0b", [P, half], F32, tag="w1_raw1_1")
+        h0b = sb("h0b", [P, half], F32, tag="w1_raw1_0")
         nc.scalar.activation(h0b[:], first_banks[2][:], GELU)
         nc.vector.tensor_copy(up[0][:].indirect(cell_sb[:, list_halves[1]]), h0b[:])
+        cast_high(nc.scalar.copy, 1, 1)
+        quantize_high(1, 1)
         h = {s: sb("h%d" % s, [P, S], F32) for s in range(1, PACK)}
         for i in range(2):
             nc.scalar.activation(h[1][:, halves[i]], h1_banks[i][:], GELU)
@@ -225,7 +214,7 @@ def tile_picked_unet_gelu_p_kernel(
         for s in range(2):
             for i in range(U // BANK):
                 cells = slice(i * BANK, (i + 1) * BANK)
-                z_low = sb("z_low%d_%d" % (s, i), [P, BANK], BF16)
+                z_low = sb("z_low%d_%d" % (s, i), [P, BANK], BF16, tag="high_in1" if (s, i) == (0, 0) else None)
                 nc.gpsimd.tensor_tensor(z_low[:], up[s][:, cells], skip_sb[s][:, cells], ADD)
                 turned = bank("turned%d_%d" % (s, i), i, blocks * P)
                 for b in range(blocks):

@@ -15,6 +15,7 @@ U8 = mybir.dt.uint8
 FP8X4 = mybir.dt.float8_e4m3fn_x4
 GELU = mybir.ActivationFunctionType.Gelu_apprx_tanh
 ADD = mybir.AluOpType.add
+MULT = mybir.AluOpType.mult
 
 P = 128
 PACK = 4
@@ -55,8 +56,8 @@ def tile_picked_unet_gelu_p_kernel(
             nc.sync.dma_start(out=table[:], in_=x_words[g].rearrange("p n t -> p (n t)").bitcast(I32))
             return table
 
-        def load_w1(side, g):
-            raw = sb("w1_raw%d_%d" % (side, g), [P, PACK, HALF_H], F32)
+        def load_w1(side, g, name=None):
+            raw = sb(name or "w1_raw%d_%d" % (side, g), [P, PACK, HALF_H], F32)
             rows = w1[g * K_PASS : (g + 1) * K_PASS, side * HALF_H : (side + 1) * HALF_H]
             nc.sync.dma_start(out=raw[:], in_=rows.rearrange("(p j) c -> p j c", j=PACK))
             return raw
@@ -75,6 +76,7 @@ def tile_picked_unet_gelu_p_kernel(
         x_table.append(load_x(1))
         nc.sync.dma_start(cell_sb[:], cell)
         w1_raw.append([load_w1(1, g) for g in range(PASSES)])
+        w1_again = load_w1(1, 1, name="w1_again")
         skip_by_slot = skip.rearrange("(m t) v -> m t v", t=PACK)
         skip_sb = {}
         for s in range(PACK):
@@ -116,10 +118,10 @@ def tile_picked_unet_gelu_p_kernel(
                 in_=w1_raw[side][g][:].rearrange("p j (m t) -> p m j t", t=PACK)[:, :, :, 0:2],
             )
 
-        def cast_high(engine_copy, side, g):
+        def cast_high(engine_copy, side, g, raw=None):
             engine_copy(
                 out=high_in[g][:].rearrange("p (e a m j) -> p a m j e", e=2, a=2, j=PACK)[:, side],
-                in_=w1_raw[side][g][:].rearrange("p j (m t) -> p m j t", t=PACK)[:, :, :, 2:4],
+                in_=(w1_raw[side][g] if raw is None else raw)[:].rearrange("p j (m t) -> p m j t", t=PACK)[:, :, :, 2:4],
             )
 
         def quantize(name, source, width, tag=None):
@@ -183,7 +185,14 @@ def tile_picked_unet_gelu_p_kernel(
             nc.scalar.activation(h0a[:, a:b], first_banks[i][:], GELU)
         nc.vector.tensor_copy(up[0][:].indirect(cell_sb[:, list_halves[0]]), h0a[:])
 
-        cast_low(nc.scalar.copy, 1, 0)
+        nc.gpsimd.tensor_scalar(
+            low_in[1][0][:].rearrange("p (m e j) -> p m e j", e=2, j=PACK),
+            w1_raw[1][0][:].rearrange("p j (m t) -> p m t j", t=PACK)[:, :, 0:2],
+            1.0,
+            0.0,
+            MULT,
+            ADD,
+        )
         cast_high(nc.scalar.copy, 1, 0)
         cast_low(nc.scalar.copy, 1, 1)
         h1_banks = [bank("h1_bank%d" % i, 3 + i, half) for i in range(2)]
@@ -193,10 +202,10 @@ def tile_picked_unet_gelu_p_kernel(
                 first_product(h1_banks[i], 1, g, halves[i])
         quantize_high(1, 0)
 
-        h0b = sb("h0b", [P, half], F32, tag="w1_raw1_0")
+        h0b = sb("h0b", [P, half], F32, tag="w1_raw1_1")
         nc.scalar.activation(h0b[:], first_banks[2][:], GELU)
         nc.vector.tensor_copy(up[0][:].indirect(cell_sb[:, list_halves[1]]), h0b[:])
-        cast_high(nc.scalar.copy, 1, 1)
+        cast_high(nc.scalar.copy, 1, 1, w1_again)
         quantize_high(1, 1)
         h = {s: sb("h%d" % s, [P, S], F32) for s in range(1, PACK)}
         for i in range(2):

@@ -1,7 +1,6 @@
 from contextlib import ExitStack
 
 import concourse.mybir as mybir
-from concourse.masks import make_identity
 
 K, T, S, H, N, U = 1024, 2048, 512, 512, 128, 1024
 FLOPS = 2 * K * H * S + 2 * H * N * U
@@ -14,21 +13,19 @@ U16 = mybir.dt.uint16
 U8 = mybir.dt.uint8
 FP8X4 = mybir.dt.float8_e4m3fn_x4
 GELU = mybir.ActivationFunctionType.Gelu_apprx_tanh
+COPY = mybir.ActivationFunctionType.Copy
 ADD = mybir.AluOpType.add
-MULT = mybir.AluOpType.mult
 
 P = 128
 PACK = 4
 K_PASS = P * PACK
 PASSES = K // K_PASS
 LIST_ROWS = 16
-HALF_H = H // 2
-M_HALF = HALF_H // PACK
-BANK = 512
-SCALAR_PIECES = [(0, 256), (256, 512), (512, 640)]
-VECTOR_CELLS = (640, U)
-WOVEN_PIECES = SCALAR_PIECES + [VECTOR_CELLS]
-PRODUCT_PIECES = [(0, 256), (640, 896), (896, U), (256, 512), (512, 640)]
+HALF = S // 2
+VECTOR_ENTRIES_3 = 128
+GPSIMD_CELLS_1 = 640
+VECTOR_CAST = 80
+PIECES = [(0, 256), (256, 512), (512, 768), (768, 1024)]
 
 
 def tile_picked_unet_gelu_p_kernel(
@@ -45,6 +42,9 @@ def tile_picked_unet_gelu_p_kernel(
         def bank(name, number, width):
             return psum.tile([P, width], F32, name=name, tag="bank%d" % number)
 
+        def entries(tile, a, b):
+            return tile[:, a // LIST_ROWS : b // LIST_ROWS]
+
         offs_sb = keep.tile([P, S // LIST_ROWS], U16, name="offs_sb")
         cell_sb = keep.tile([P, S // LIST_ROWS], U16, name="cell_sb")
 
@@ -56,36 +56,31 @@ def tile_picked_unet_gelu_p_kernel(
             nc.sync.dma_start(out=table[:], in_=x_words[g].rearrange("p n t -> p (n t)").bitcast(I32))
             return table
 
-        def load_w1(side, g, name=None):
-            raw = sb(name or "w1_raw%d_%d" % (side, g), [P, PACK, HALF_H], F32)
-            rows = w1[g * K_PASS : (g + 1) * K_PASS, side * HALF_H : (side + 1) * HALF_H]
-            nc.sync.dma_start(out=raw[:], in_=rows.rearrange("(p j) c -> p j c", j=PACK))
-            return raw
+        w1_raw = [sb("w1_raw%d" % g, [P, PACK, H], F32) for g in range(PASSES)]
 
-        w1_raw = [[load_w1(0, 0)]]
-        nc.sync.dma_start(offs_sb[:], offs)
+        def load_w1(g, first, last):
+            rows = w1[g * K_PASS : (g + 1) * K_PASS, :].rearrange("(p j) c -> p j c", j=PACK)
+            nc.sync.dma_start(out=w1_raw[g][:, first:last, :], in_=rows[:, first:last, :])
 
         def load_x_scales(g):
             for r in range(4):
                 nc.sync.dma_start(out=x_scale_table[4 * g + r : P : 32, :].bitcast(I32), in_=x_scales[g, r:16:4, :].bitcast(I32))
 
+        load_w1(0, 0, 2)
+        nc.sync.dma_start(offs_sb[:], offs)
         load_x_scales(0)
+        load_w1(0, 2, PACK)
         x_table = [load_x(0)]
         load_x_scales(1)
-        w1_raw[0].append(load_w1(0, 1))
+        load_w1(1, 0, PACK)
         x_table.append(load_x(1))
         nc.sync.dma_start(cell_sb[:], cell)
-        w1_raw.append([load_w1(1, g) for g in range(PASSES)])
-        w1_again = load_w1(1, 1, name="w1_again")
         skip_by_slot = skip.rearrange("(m t) v -> m t v", t=PACK)
-        skip_sb = {}
-        for s in range(PACK):
-            plane = sb("skip%d" % s, [P, U], F32)
-            if s < 2:
-                nc.sync.dma_start(out=plane[:], in_=skip_by_slot[s * M_HALF : (s + 1) * M_HALF, 0:2, :])
-            else:
-                nc.sync.dma_start(out=plane[:], in_=skip_by_slot[:, s, :])
-            skip_sb[s] = plane
+        skip_sb = []
+        for t in range(PACK):
+            plane = sb("skip%d" % t, [P, U], F32)
+            nc.sync.dma_start(out=plane[:], in_=skip_by_slot[:, t, :])
+            skip_sb.append(plane)
         w2_codes = sb("w2_codes", [P, N], I32)
         nc.sync.dma_start(out=w2_codes[:], in_=w2_words[0].rearrange("p n t -> p (n t)").bitcast(I32))
         w2_plane = sb("w2_plane", [P, N], U8)
@@ -93,181 +88,106 @@ def tile_picked_unet_gelu_p_kernel(
         for r in range(4):
             nc.sync.dma_start(out=w2_plane[r:P:32, :].bitcast(I32), in_=w2_scales[0, r:16:4, :].bitcast(I32))
 
-        up = [sb("up%d" % s, [P, U], F32) for s in range(PACK)]
+        up = [sb("up%d" % t, [P, U], F32) for t in range(PACK)]
         nc.vector.memset(up[1][:], 0.0)
         nc.scalar.activation(up[0][:], up[1][:], GELU)
-        for s in range(2, PACK):
-            nc.gpsimd.memset(up[s][:], 0.0)
-        ident = sb("ident", [P, P], F32)
-        make_identity(nc, ident[:])
+        for t in range(2, PACK):
+            nc.gpsimd.memset(up[t][:], 0.0)
 
-        half = S // 2
-        halves = [slice(0, half), slice(half, S)]
-        list_halves = [slice(0, half // LIST_ROWS), slice(half // LIST_ROWS, S // LIST_ROWS)]
+        def quantize(name, source, width):
+            codes = sb(name + "_codes", [P, width], U32)
+            plane = sb(name + "_plane", [P, width], U8)
+            nc.vector.quantize_mx(out=codes[:].bitcast(FP8X4), scales=plane[:], in_=source)
+            return codes, plane
+
+        w1_grouped = [sb("w1_grouped%d" % g, [P, H * PACK], BF16) for g in range(PASSES)]
+
+        def cast_w1(engine_copy, g, first, last):
+            engine_copy(
+                out=w1_grouped[g][:].rearrange("p (t m j) -> p m j t", t=PACK, j=PACK)[:, first:last],
+                in_=w1_raw[g][:].rearrange("p j (m t) -> p m j t", t=PACK)[:, first:last],
+            )
+
+        cast_w1(nc.vector.tensor_copy, 0, 0, P)
+        w1_mx = [quantize("w1_0", w1_grouped[0][:], H)]
 
         x_codes = [sb("x_codes%d" % g, [P, S], U32) for g in range(PASSES)]
         x_plane = sb("x_plane", [P, S], U8)
+        nc.vector.tensor_copy(x_codes[0][:], x_table[0][:].bitcast(U32).indirect(offs_sb[:]))
+        nc.vector.tensor_copy(x_plane[:], x_scale_table[:].indirect(offs_sb[:]))
+        cast_w1(nc.vector.tensor_copy, 1, 0, VECTOR_CAST)
+        cast_w1(nc.scalar.copy, 1, VECTOR_CAST, P)
+        w1_mx.append(quantize("w1_1", w1_grouped[1][:], H))
 
-        low_in = [[sb("low_in%d_%d" % (side, g), [P, P * PACK], BF16) for g in range(PASSES)] for side in range(2)]
-        high_in = [sb("high_in%d" % g, [P, 2 * P * PACK], BF16) for g in range(PASSES)]
-        codes, planes = {}, {}
-
-        def cast_low(engine_copy, side, g):
-            engine_copy(
-                out=low_in[side][g][:].rearrange("p (m e j) -> p m j e", e=2, j=PACK),
-                in_=w1_raw[side][g][:].rearrange("p j (m t) -> p m j t", t=PACK)[:, :, :, 0:2],
-            )
-
-        def cast_high(engine_copy, side, g, raw=None):
-            engine_copy(
-                out=high_in[g][:].rearrange("p (e a m j) -> p a m j e", e=2, a=2, j=PACK)[:, side],
-                in_=(w1_raw[side][g] if raw is None else raw)[:].rearrange("p j (m t) -> p m j t", t=PACK)[:, :, :, 2:4],
-            )
-
-        def quantize(name, source, width, tag=None):
-            c = sb(name + "_codes", [P, width], U32, tag=tag)
-            pl = sb(name + "_plane", [P, width], U8)
-            nc.vector.quantize_mx(out=c[:].bitcast(FP8X4), scales=pl[:], in_=source)
-            return c, pl
-
-        def quantize_low(side, g, tag=None):
-            c, pl = quantize("low%d_%d" % (side, g), low_in[side][g][:], P, tag=tag)
-            codes[side, g], planes[side, g] = c[:], pl[:]
-
-        high_codes = [sb("high_codes%d" % g, [P, 2 * P], U32) for g in range(PASSES)]
-        high_plane = [sb("high_plane%d" % g, [P, 2 * P], U8) for g in range(PASSES)]
-        for g in range(PASSES):
-            for e in range(2):
-                codes[2 + e, g] = high_codes[g][:, e * P : (e + 1) * P]
-                planes[2 + e, g] = high_plane[g][:, e * P : (e + 1) * P]
-
-        def quantize_high(side, g):
-            for e in range(2):
-                first = e * P + side * M_HALF
-                nc.vector.quantize_mx(
-                    out=high_codes[g][:, first : first + M_HALF].bitcast(FP8X4),
-                    scales=high_plane[g][:, first : first + M_HALF],
-                    in_=high_in[g][:, first * PACK : (first + M_HALF) * PACK],
-                )
-
-        def first_product(acc, s, g, cols):
+        def first_product(acc, t, g, a, b):
+            codes, plane = w1_mx[g]
             nc.tensor.matmul_mx(
                 out=acc[:],
-                lhsT=codes[s, g].bitcast(FP8X4),
-                lhsT_scale=planes[s, g],
-                rhs=x_codes[g][:, cols].bitcast(FP8X4),
-                rhs_scale=x_plane[4 * g : P, cols],
+                lhsT=codes[:, t * P : (t + 1) * P].bitcast(FP8X4),
+                lhsT_scale=plane[:, t * P : (t + 1) * P],
+                rhs=x_codes[g][:, a:b].bitcast(FP8X4),
+                rhs_scale=x_plane[4 * g : P, a:b],
                 start=(g == 0),
                 stop=(g == PASSES - 1),
             )
 
-        for g in range(PASSES):
-            cast_low(nc.scalar.copy, 0, g)
-            cast_high(nc.scalar.copy, 0, g)
-        quantize_low(0, 0)
-        nc.vector.tensor_copy(x_codes[0][:], x_table[0][:].bitcast(U32).indirect(offs_sb[:]))
-        nc.vector.tensor_copy(x_plane[:], x_scale_table[:].indirect(offs_sb[:]))
-        quantize_low(0, 1)
-        for g in range(PASSES):
-            quantize_high(0, g)
-        first_pieces = [(0, 128), (128, 256), (256, S)]
-        first_banks = [bank("h0_bank%d" % i, i, b - a) for i, (a, b) in enumerate(first_pieces)]
-        for i, (a, b) in enumerate(first_pieces):
-            first_product(first_banks[i], 0, 0, slice(a, b))
-        for i in range(2):
-            nc.vector.tensor_copy(x_codes[1][:, halves[i]], x_table[1][:].bitcast(U32).indirect(offs_sb[:, list_halves[i]]))
-        for i, (a, b) in enumerate(first_pieces):
-            first_product(first_banks[i], 0, 1, slice(a, b))
+        parts = [(3, 0, HALF), (0, 0, HALF), (1, 0, HALF), (0, HALF, S), (1, HALF, S), (2, 0, S), (3, HALF, S)]
+        banks = [bank("h_bank%d" % i, i, b - a) for i, (t, a, b) in enumerate(parts)]
+        for i, (t, a, b) in enumerate(parts):
+            first_product(banks[i], t, 0, a, b)
+        for a, b in ((0, HALF), (HALF, S)):
+            nc.vector.tensor_copy(x_codes[1][:, a:b], x_table[1][:].bitcast(U32).indirect(entries(offs_sb, a, b)))
+        for i, (t, a, b) in enumerate(parts):
+            first_product(banks[i], t, 1, a, b)
 
-        h0a = sb("h0a", [P, half], F32)
-        for i in range(2):
-            a, b = first_pieces[i]
-            nc.scalar.activation(h0a[:, a:b], first_banks[i][:], GELU)
-        nc.vector.tensor_copy(up[0][:].indirect(cell_sb[:, list_halves[0]]), h0a[:])
+        h = [sb("h%d" % t, [P, S], F32) for t in range(PACK)]
 
-        nc.gpsimd.tensor_scalar(
-            low_in[1][0][:].rearrange("p (m e j) -> p m e j", e=2, j=PACK),
-            w1_raw[1][0][:].rearrange("p j (m t) -> p m t j", t=PACK)[:, :, 0:2],
-            1.0,
-            0.0,
-            MULT,
-            ADD,
-        )
-        cast_high(nc.scalar.copy, 1, 0)
-        cast_low(nc.scalar.copy, 1, 1)
-        h1_banks = [bank("h1_bank%d" % i, 3 + i, half) for i in range(2)]
-        for g in range(PASSES):
-            quantize_low(1, g)
-            for i in range(2):
-                first_product(h1_banks[i], 1, g, halves[i])
-        quantize_high(1, 0)
+        def gelu(i):
+            t, a, b = parts[i]
+            nc.scalar.activation(h[t][:, a:b], banks[i][:], GELU)
 
-        h0b = sb("h0b", [P, half], F32, tag="w1_raw1_1")
-        nc.scalar.activation(h0b[:], first_banks[2][:], GELU)
-        nc.vector.tensor_copy(up[0][:].indirect(cell_sb[:, list_halves[1]]), h0b[:])
-        cast_high(nc.scalar.copy, 1, 1, w1_again)
-        quantize_high(1, 1)
-        h = {s: sb("h%d" % s, [P, S], F32) for s in range(1, PACK)}
-        for i in range(2):
-            nc.scalar.activation(h[1][:, halves[i]], h1_banks[i][:], GELU)
-        for s in range(2, PACK):
-            acc = bank("h%d_bank" % s, s + 1, S)
-            for g in range(PASSES):
-                first_product(acc, s, g, slice(0, S))
-            nc.scalar.activation(h[s][:], acc[:], GELU)
-        for s in range(1, PACK):
-            nc.vector.tensor_copy(up[s][:].indirect(cell_sb[:]), h[s][:])
+        def scatter_vector(t, a, b):
+            nc.vector.tensor_copy(up[t][:].indirect(entries(cell_sb, a, b)), h[t][:, a:b])
 
-        blocks = BANK // (2 * P)
-        z_turned = [sb("z_turned%d" % i, [P, blocks, 2, 2, P], BF16) for i in range(U // BANK)]
-        for s in range(2):
-            for i in range(U // BANK):
-                cells = slice(i * BANK, (i + 1) * BANK)
-                z_low = sb("z_low%d_%d" % (s, i), [P, BANK], BF16, tag="high_in1" if (s, i) == (0, 0) else None)
-                nc.gpsimd.tensor_tensor(z_low[:], up[s][:, cells], skip_sb[s][:, cells], ADD)
-                turned = bank("turned%d_%d" % (s, i), i, blocks * P)
-                for b in range(blocks):
-                    nc.tensor.transpose(turned[:, b * P : (b + 1) * P], z_low[:].bitcast(F32)[:, b * P : (b + 1) * P], ident[:])
-                nc.scalar.copy(
-                    out=z_turned[i][:, :, :, s, :],
-                    in_=turned[:].bitcast(BF16).rearrange("p (b q c) -> p b c q", b=blocks, c=2),
-                )
+        def scatter_scalar(t, a, b):
+            nc.scalar.activation(up[t][:].indirect(entries(cell_sb, a, b)), h[t][:, a:b], COPY)
 
-        z_grouped = {a: sb("z_grouped%d" % a, [P, (b - a) * PACK], BF16) for a, b in WOVEN_PIECES}
-        for i in range(U // BANK):
-            back = bank("back%d" % i, 3 + i, BANK)
-            for b in range(blocks):
-                for c in range(2):
-                    words = z_turned[i][:, b, c].rearrange("p s q -> p (s q)").bitcast(F32)
-                    nc.tensor.transpose(back[:, (2 * b + c) * P : (2 * b + c + 1) * P], words, ident[:])
-            by_cell = back[:].rearrange("p (b c j) -> p b j c", b=blocks, c=2)
-            for a, b in WOVEN_PIECES:
-                for first in range(i * BANK, (i + 1) * BANK, 2 * P):
-                    lo, hi = max(a, first), min(b, first + 2 * P)
-                    if lo < hi:
-                        source = by_cell[:, (first - i * BANK) // (2 * P), (lo - first) // 2 : (hi - first) // 2]
-                        nc.scalar.copy(
-                            out=z_grouped[a][:].bitcast(F32)[:, 2 * (lo - a) : 2 * (hi - a)].rearrange("p (j c u) -> p j c u", c=2, u=2),
-                            in_=source.unsqueeze(3).to_broadcast([P, (hi - lo) // 2, 2, 2]),
-                        )
+        for i in range(5):
+            gelu(i)
+        scatter_vector(3, 0, VECTOR_ENTRIES_3)
+        scatter_vector(0, 0, S)
+        scatter_scalar(1, HALF, S)
+        gelu(5)
+        gelu(6)
+        scatter_scalar(1, 0, HALF)
+        scatter_vector(2, 0, S)
+        scatter_scalar(3, VECTOR_ENTRIES_3, S)
 
-        z_high = sb("z_high", [P, 2, U], BF16)
-        nc.gpsimd.tensor_tensor(z_high[:, 0, :], up[2][:], skip_sb[2][:], ADD)
-        for a, b in [(0, 256), VECTOR_CELLS, (256, 640)]:
-            nc.vector.tensor_tensor(z_high[:, 1, a:b], up[3][:, a:b], skip_sb[3][:, a:b], ADD)
+        z = sb("z", [P, PACK, U], BF16)
 
-        def weave(engine_copy, a, b):
+        def add_skip(engine, t, a, b):
+            engine.tensor_tensor(z[:, t, a:b], up[t][:, a:b], skip_sb[t][:, a:b], ADD)
+
+        add_skip(nc.gpsimd, 0, 0, U)
+        add_skip(nc.gpsimd, 1, 0, GPSIMD_CELLS_1)
+        add_skip(nc.vector, 1, GPSIMD_CELLS_1, U)
+        for a, b in PIECES:
+            add_skip(nc.vector, 2, a, b)
+            add_skip(nc.vector, 3, a, b)
+
+        z_grouped = [sb("z_grouped%d" % a, [P, (b - a) * PACK], BF16) for a, b in PIECES]
+
+        def weave(engine_copy, i):
+            a, b = PIECES[i]
             engine_copy(
-                out=z_grouped[a][:].rearrange("p (c e u t) -> p u c t e", e=4, u=2, t=2)[:, 1],
-                in_=z_high[:, :, a:b].rearrange("p t (c e) -> p c t e", e=4),
+                out=z_grouped[i][:].rearrange("p (c e t) -> p c t e", e=4, t=PACK),
+                in_=z[:, :, a:b].rearrange("p t (c e) -> p c t e", e=4),
             )
 
-        def second_product(i, engine_copy):
-            a, b = PRODUCT_PIECES[i]
-            start = max(first for first, last in WOVEN_PIECES if first <= a)
-            source = z_grouped[start][:, (a - start) * PACK : (b - start) * PACK]
-            z_codes, z_plane = quantize("z%d" % a, source, b - a)
-            acc = bank("out_bank%d" % i, (5, 6, 7, 1, 2)[i], b - a)
+        def second_product(i, number, engine_copy):
+            a, b = PIECES[i]
+            z_codes, z_plane = quantize("z%d" % a, z_grouped[i][:], b - a)
+            acc = bank("out_bank%d" % i, number, b - a)
             nc.tensor.matmul_mx(
                 out=acc[:],
                 lhsT=w2_codes[:].bitcast(FP8X4),
@@ -281,11 +201,10 @@ def tile_picked_unet_gelu_p_kernel(
             engine_copy(out=result[:], in_=acc[:])
             nc.sync.dma_start(out=out[:, a:b], in_=result[:])
 
-        for a, b in SCALAR_PIECES:
-            weave(nc.scalar.copy, a, b)
-        weave(nc.vector.tensor_copy, *VECTOR_CELLS)
-        second_product(0, nc.scalar.copy)
-        second_product(1, nc.scalar.copy)
-        second_product(2, nc.scalar.copy)
-        second_product(3, nc.scalar.copy)
-        second_product(4, nc.vector.tensor_copy)
+        for i in range(3):
+            weave(nc.scalar.copy, i)
+        weave(nc.vector.tensor_copy, 3)
+        second_product(0, 7, nc.scalar.copy)
+        second_product(3, 0, nc.scalar.copy)
+        second_product(1, 1, nc.scalar.copy)
+        second_product(2, 2, nc.vector.tensor_copy)

@@ -22,10 +22,10 @@ K_PASS = P * PACK
 PASSES = K // K_PASS
 LIST_ROWS = 16
 HALF = S // 2
-VECTOR_ENTRIES_3 = 128
-GPSIMD_CELLS_1 = 640
+QUARTER = S // 4
 VECTOR_CAST = 80
-PIECES = [(0, 256), (256, 512), (512, 768), (768, 1024)]
+PIECES = [(0, 256), (256, 512), (512, 768), (768, U)]
+ADD_PIECES = [(0, 256), (512, U), (256, 512)]
 
 
 def tile_picked_unet_gelu_p_kernel(
@@ -131,11 +131,11 @@ def tile_picked_unet_gelu_p_kernel(
                 stop=(g == PASSES - 1),
             )
 
-        parts = [(3, 0, HALF), (0, 0, HALF), (1, 0, HALF), (0, HALF, S), (1, HALF, S), (2, 0, S), (3, HALF, S)]
+        parts = [(0, 0, QUARTER), (0, QUARTER, HALF), (2, 0, HALF), (1, 0, HALF), (0, HALF, S), (1, HALF, S), (2, HALF, S), (3, 0, S)]
         banks = [bank("h_bank%d" % i, i, b - a) for i, (t, a, b) in enumerate(parts)]
         for i, (t, a, b) in enumerate(parts):
             first_product(banks[i], t, 0, a, b)
-        for a, b in ((0, HALF), (HALF, S)):
+        for a, b in ((0, QUARTER), (QUARTER, HALF), (HALF, S)):
             nc.vector.tensor_copy(x_codes[1][:, a:b], x_table[1][:].bitcast(U32).indirect(entries(offs_sb, a, b)))
         for i, (t, a, b) in enumerate(parts):
             first_product(banks[i], t, 1, a, b)
@@ -152,16 +152,18 @@ def tile_picked_unet_gelu_p_kernel(
         def scatter_scalar(t, a, b):
             nc.scalar.activation(up[t][:].indirect(entries(cell_sb, a, b)), h[t][:, a:b], COPY)
 
-        for i in range(5):
+        for i in range(6):
             gelu(i)
-        scatter_vector(3, 0, VECTOR_ENTRIES_3)
-        scatter_vector(0, 0, S)
+        scatter_vector(0, 0, HALF)
+        scatter_vector(2, 0, QUARTER)
+        scatter_vector(0, HALF, S)
         scatter_scalar(1, HALF, S)
-        gelu(5)
         gelu(6)
+        gelu(7)
+        scatter_vector(2, QUARTER, S)
+        scatter_scalar(3, 0, QUARTER)
         scatter_scalar(1, 0, HALF)
-        scatter_vector(2, 0, S)
-        scatter_scalar(3, VECTOR_ENTRIES_3, S)
+        scatter_scalar(3, QUARTER, S)
 
         z = sb("z", [P, PACK, U], BF16)
 
@@ -169,24 +171,22 @@ def tile_picked_unet_gelu_p_kernel(
             engine.tensor_tensor(z[:, t, a:b], up[t][:, a:b], skip_sb[t][:, a:b], ADD)
 
         add_skip(nc.gpsimd, 0, 0, U)
-        add_skip(nc.gpsimd, 1, 0, GPSIMD_CELLS_1)
-        add_skip(nc.vector, 1, GPSIMD_CELLS_1, U)
-        for a, b in PIECES:
-            add_skip(nc.vector, 2, a, b)
+        add_skip(nc.vector, 1, 0, U)
+        add_skip(nc.vector, 2, 0, U)
+        for a, b in ADD_PIECES:
             add_skip(nc.vector, 3, a, b)
 
-        z_grouped = [sb("z_grouped%d" % a, [P, (b - a) * PACK], BF16) for a, b in PIECES]
+        z_grouped = {a: sb("z_grouped%d" % a, [P, (b - a) * PACK], BF16) for a, b in PIECES}
 
-        def weave(engine_copy, i):
-            a, b = PIECES[i]
+        def weave(engine_copy, a, b):
             engine_copy(
-                out=z_grouped[i][:].rearrange("p (c e t) -> p c t e", e=4, t=PACK),
+                out=z_grouped[a][:].rearrange("p (c e t) -> p c t e", e=4, t=PACK),
                 in_=z[:, :, a:b].rearrange("p t (c e) -> p c t e", e=4),
             )
 
         def second_product(i, number, engine_copy):
             a, b = PIECES[i]
-            z_codes, z_plane = quantize("z%d" % a, z_grouped[i][:], b - a)
+            z_codes, z_plane = quantize("z%d" % a, z_grouped[a][:], b - a)
             acc = bank("out_bank%d" % i, number, b - a)
             nc.tensor.matmul_mx(
                 out=acc[:],
@@ -201,10 +201,11 @@ def tile_picked_unet_gelu_p_kernel(
             engine_copy(out=result[:], in_=acc[:])
             nc.sync.dma_start(out=out[:, a:b], in_=result[:])
 
-        for i in range(3):
-            weave(nc.scalar.copy, i)
-        weave(nc.vector.tensor_copy, 3)
+        weave(nc.scalar.copy, *PIECES[0])
+        weave(nc.scalar.copy, *PIECES[1])
+        weave(nc.vector.tensor_copy, *PIECES[2])
         second_product(0, 7, nc.scalar.copy)
-        second_product(3, 0, nc.scalar.copy)
-        second_product(1, 1, nc.scalar.copy)
-        second_product(2, 2, nc.vector.tensor_copy)
+        weave(nc.vector.tensor_copy, *PIECES[3])
+        second_product(2, 0, nc.scalar.copy)
+        second_product(3, 1, nc.scalar.copy)
+        second_product(1, 2, nc.vector.tensor_copy)

@@ -23,7 +23,6 @@ PASSES = K // K_PASS
 LIST_ROWS = 16
 HALF = S // 2
 QUARTER = S // 4
-VECTOR_CAST = 80
 PIECES = [(0, 256), (256, 512), (512, 768), (768, U)]
 ADD_PIECES = [(0, 256), (512, U), (256, 512)]
 
@@ -104,23 +103,33 @@ def tile_picked_unet_gelu_p_kernel(
 
         def cast_w1(engine_copy, g, first, last):
             engine_copy(
-                out=w1_grouped[g][:].rearrange("p (t m j) -> p m j t", t=PACK, j=PACK)[:, first:last],
-                in_=w1_raw[g][:].rearrange("p j (m t) -> p m j t", t=PACK)[:, first:last],
+                out=w1_grouped[g][:].rearrange("p (t m j) -> p m j t", t=PACK, j=PACK)[:, :, :, first:last],
+                in_=w1_raw[g][:].rearrange("p j (m t) -> p m j t", t=PACK)[:, :, :, first:last],
             )
 
-        cast_w1(nc.vector.tensor_copy, 0, 0, P)
-        w1_mx = [quantize("w1_0", w1_grouped[0][:], H)]
+        w1_codes = [sb("w1_codes%d" % g, [P, H], U32) for g in range(PASSES)]
+        w1_plane = [sb("w1_plane%d" % g, [P, H], U8) for g in range(PASSES)]
+
+        def prepare_w1(g):
+            cast_w1(nc.vector.tensor_copy, g, 0, 2)
+            cast_w1(nc.scalar.copy, g, 2, PACK)
+            for first in (0, H // 2):
+                nc.vector.quantize_mx(
+                    out=w1_codes[g][:, first : first + H // 2].bitcast(FP8X4),
+                    scales=w1_plane[g][:, first : first + H // 2],
+                    in_=w1_grouped[g][:, first * PACK : (first + H // 2) * PACK],
+                )
+
+        prepare_w1(0)
 
         x_codes = [sb("x_codes%d" % g, [P, S], U32) for g in range(PASSES)]
         x_plane = sb("x_plane", [P, S], U8)
         nc.vector.tensor_copy(x_codes[0][:], x_table[0][:].bitcast(U32).indirect(offs_sb[:]))
         nc.vector.tensor_copy(x_plane[:], x_scale_table[:].indirect(offs_sb[:]))
-        cast_w1(nc.vector.tensor_copy, 1, 0, VECTOR_CAST)
-        cast_w1(nc.scalar.copy, 1, VECTOR_CAST, P)
-        w1_mx.append(quantize("w1_1", w1_grouped[1][:], H))
+        prepare_w1(1)
 
         def first_product(acc, t, g, a, b):
-            codes, plane = w1_mx[g]
+            codes, plane = w1_codes[g], w1_plane[g]
             nc.tensor.matmul_mx(
                 out=acc[:],
                 lhsT=codes[:, t * P : (t + 1) * P].bitcast(FP8X4),
@@ -131,7 +140,7 @@ def tile_picked_unet_gelu_p_kernel(
                 stop=(g == PASSES - 1),
             )
 
-        parts = [(0, 0, QUARTER), (0, QUARTER, HALF), (2, 0, HALF), (1, 0, HALF), (0, HALF, S), (1, HALF, S), (2, HALF, S), (3, 0, S)]
+        parts = [(0, 0, QUARTER), (0, QUARTER, HALF), (3, 0, HALF), (1, 0, HALF), (2, 0, S), (0, HALF, S), (1, HALF, S), (3, HALF, S)]
         banks = [bank("h_bank%d" % i, i, b - a) for i, (t, a, b) in enumerate(parts)]
         for i, (t, a, b) in enumerate(parts):
             first_product(banks[i], t, 0, a, b)
@@ -152,18 +161,12 @@ def tile_picked_unet_gelu_p_kernel(
         def scatter_scalar(t, a, b):
             nc.scalar.activation(up[t][:].indirect(entries(cell_sb, a, b)), h[t][:, a:b], COPY)
 
-        for i in range(6):
+        for i in range(len(parts)):
             gelu(i)
-        scatter_vector(0, 0, HALF)
-        scatter_vector(2, 0, QUARTER)
-        scatter_vector(0, HALF, S)
-        scatter_scalar(1, HALF, S)
-        gelu(6)
-        gelu(7)
-        scatter_vector(2, QUARTER, S)
-        scatter_scalar(3, 0, QUARTER)
-        scatter_scalar(1, 0, HALF)
-        scatter_scalar(3, QUARTER, S)
+        for t, split in ((0, HALF), (3, QUARTER), (1, QUARTER), (2, S)):
+            scatter_vector(t, 0, split)
+        for t, split in ((0, HALF), (1, QUARTER), (3, QUARTER)):
+            scatter_scalar(t, split, S)
 
         z = sb("z", [P, PACK, U], BF16)
 

@@ -140,7 +140,7 @@ def tile_picked_unet_gelu_p_kernel(
                 stop=(g == PASSES - 1),
             )
 
-        parts = [(0, 0, QUARTER), (0, QUARTER, HALF), (3, 0, HALF), (1, 0, HALF), (2, 0, S), (0, HALF, S), (1, HALF, S), (3, HALF, S)]
+        parts = [(0, 0, QUARTER), (1, 0, HALF), (0, QUARTER, HALF), (3, 0, HALF), (0, HALF, S), (2, 0, S), (1, HALF, S), (3, HALF, S)]
         banks = [bank("h_bank%d" % i, i, b - a) for i, (t, a, b) in enumerate(parts)]
         for i, (t, a, b) in enumerate(parts):
             first_product(banks[i], t, 0, a, b)
@@ -161,12 +161,15 @@ def tile_picked_unet_gelu_p_kernel(
         def scatter_scalar(t, a, b):
             nc.scalar.activation(up[t][:].indirect(entries(cell_sb, a, b)), h[t][:, a:b], COPY)
 
-        for i in range(len(parts)):
+        for i in range(6):
             gelu(i)
-        for t, split in ((0, HALF), (3, QUARTER), (1, QUARTER), (2, S)):
+        for t, split in ((0, QUARTER), (1, HALF), (3, QUARTER), (2, S)):
             scatter_vector(t, 0, split)
-        for t, split in ((0, HALF), (1, QUARTER), (3, QUARTER)):
-            scatter_scalar(t, split, S)
+        scatter_scalar(0, QUARTER, S)
+        gelu(6)
+        gelu(7)
+        scatter_scalar(1, HALF, S)
+        scatter_scalar(3, QUARTER, S)
 
         z = sb("z", [P, PACK, U], BF16)
 

@@ -24,6 +24,7 @@ LIST_ROWS = 16
 HALF = S // 2
 QUARTER = S // 4
 PIECES = [(0, 256), (256, 512), (512, 768), (768, U)]
+EARLY = 6
 ADD_PIECES = [(0, 256), (512, U), (256, 512)]
 
 
@@ -128,7 +129,7 @@ def tile_picked_unet_gelu_p_kernel(
         nc.vector.tensor_copy(x_plane[:], x_scale_table[:].indirect(offs_sb[:]))
         prepare_w1(1)
 
-        def first_product(acc, t, g, a, b):
+        def first_product(acc, t, g, a, b, start):
             codes, plane = w1_codes[g], w1_plane[g]
             nc.tensor.matmul_mx(
                 out=acc[:],
@@ -136,18 +137,21 @@ def tile_picked_unet_gelu_p_kernel(
                 lhsT_scale=plane[:, t * P : (t + 1) * P],
                 rhs=x_codes[g][:, a:b].bitcast(FP8X4),
                 rhs_scale=x_plane[4 * g : P, a:b],
-                start=(g == 0),
-                stop=(g == PASSES - 1),
+                start=start,
+                stop=not start,
             )
 
         parts = [(0, 0, QUARTER), (1, 0, HALF), (0, QUARTER, HALF), (3, 0, HALF), (0, HALF, S), (2, 0, S), (1, HALF, S), (3, HALF, S)]
         banks = [bank("h_bank%d" % i, i, b - a) for i, (t, a, b) in enumerate(parts)]
-        for i, (t, a, b) in enumerate(parts):
-            first_product(banks[i], t, 0, a, b)
+        for i, (t, a, b) in enumerate(parts[:EARLY]):
+            first_product(banks[i], t, 0, a, b, True)
         for a, b in ((0, QUARTER), (QUARTER, HALF), (HALF, S)):
             nc.vector.tensor_copy(x_codes[1][:, a:b], x_table[1][:].bitcast(U32).indirect(entries(offs_sb, a, b)))
         for i, (t, a, b) in enumerate(parts):
-            first_product(banks[i], t, 1, a, b)
+            first_product(banks[i], t, 1, a, b, i >= EARLY)
+        for i, (t, a, b) in enumerate(parts):
+            if i >= EARLY:
+                first_product(banks[i], t, 0, a, b, False)
 
         h = [sb("h%d" % t, [P, S], F32) for t in range(PACK)]
 

@@ -62,8 +62,8 @@ def tile_picked_unet_gelu_p_kernel(
             rows = w1[g * K_PASS : (g + 1) * K_PASS, :].rearrange("(p j) c -> p j c", j=PACK)
             nc.sync.dma_start(out=w1_raw[g][:, first:last, :], in_=rows[:, first:last, :])
 
-        def load_x_scales(g):
-            for r in range(4):
+        def load_x_scales(first):
+            for r, g in ((first, 0), (first, 1), (first + 1, 0), (first + 1, 1)):
                 nc.sync.dma_start(out=x_scale_table[4 * g + r : P : 32, :].bitcast(I32), in_=x_scales[g, r:16:4, :].bitcast(I32))
 
         load_w1(0, 0, 2)
@@ -71,7 +71,7 @@ def tile_picked_unet_gelu_p_kernel(
         load_x_scales(0)
         load_w1(0, 2, PACK)
         x_table = [load_x(0)]
-        load_x_scales(1)
+        load_x_scales(2)
         load_w1(1, 0, PACK)
         x_table.append(load_x(1))
         nc.sync.dma_start(cell_sb[:], cell)

@@ -1,6 +1,7 @@
 from contextlib import ExitStack
 
 import concourse.mybir as mybir
+from concourse.masks import make_identity
 
 K, T, S, H, N, U = 1024, 2048, 512, 512, 128, 1024
 FLOPS = 2 * K * H * S + 2 * H * N * U
@@ -25,7 +26,7 @@ HALF = S // 2
 QUARTER = S // 4
 PIECES = [(0, 256), (256, 512), (512, 768), (768, U)]
 EARLY = 6
-ADD_PIECES = [(0, 256), (512, U), (256, 512)]
+TURNED = 3 * P
 
 
 def tile_picked_unet_gelu_p_kernel(
@@ -93,6 +94,9 @@ def tile_picked_unet_gelu_p_kernel(
         nc.scalar.activation(up[0][:], up[1][:], GELU)
         for t in range(2, PACK):
             nc.gpsimd.memset(up[t][:], 0.0)
+
+        identity = sb("identity", [P, P], F32)
+        make_identity(nc, identity[:])
 
         def quantize(name, source, width):
             codes = sb(name + "_codes", [P, width], U32)
@@ -167,31 +171,74 @@ def tile_picked_unet_gelu_p_kernel(
 
         for i in range(6):
             gelu(i)
-        for t, split in ((0, QUARTER), (1, HALF), (3, QUARTER), (2, S)):
+        for t, split in ((0, QUARTER), (1, HALF), (3, HALF), (2, S)):
             scatter_vector(t, 0, split)
         scatter_scalar(0, QUARTER, S)
         gelu(6)
         gelu(7)
         scatter_scalar(1, HALF, S)
-        scatter_scalar(3, QUARTER, S)
+        scatter_scalar(3, HALF, S)
 
-        z = sb("z", [P, PACK, U], BF16)
+        spans = [(0, 2), (2, 3)]
+        sum_banks = {(u, i): bank("sum_bank%d%d" % (u, i), 2 * u + i, (b - a) * 2 * P) for u in range(2) for i, (a, b) in enumerate(spans)}
+
+        def turn(source, t, opens, closes):
+            for i, (first, last) in enumerate(spans):
+                for block in range(first, last):
+                    column = ((block - first) * 2 + t % 2) * P
+                    nc.tensor.matmul(
+                        sum_banks[(t // 2, i)][:, column : column + P],
+                        lhsT=source[:, block * P : (block + 1) * P],
+                        rhs=identity[:],
+                        start=opens and block == first,
+                        stop=closes and block == last - 1,
+                        is_transpose=True,
+                    )
+
+        for t in range(PACK):
+            turn(skip_sb[t], t, t % 2 == 0, False)
+        for t in (0, 1, 2, 3):
+            turn(up[t], t, False, t % 2 == 1)
+
+        z = sb("z", [P, PACK, U - TURNED], BF16)
 
         def add_skip(engine, t, a, b):
-            engine.tensor_tensor(z[:, t, a:b], up[t][:, a:b], skip_sb[t][:, a:b], ADD)
+            engine.tensor_tensor(z[:, t, a - TURNED : b - TURNED], up[t][:, a:b], skip_sb[t][:, a:b], ADD)
 
-        add_skip(nc.gpsimd, 0, 0, U)
-        add_skip(nc.vector, 1, 0, U)
-        add_skip(nc.vector, 2, 0, U)
-        for a, b in ADD_PIECES:
-            add_skip(nc.vector, 3, a, b)
+        add_skip(nc.gpsimd, 0, TURNED, U)
+        add_skip(nc.gpsimd, 1, 512, U)
+        add_skip(nc.vector, 1, TURNED, 512)
+        add_skip(nc.vector, 2, TURNED, U)
+        add_skip(nc.vector, 3, 512, 768)
+        add_skip(nc.vector, 3, 768, U)
+        add_skip(nc.vector, 3, TURNED, 512)
 
         z_grouped = {a: sb("z_grouped%d" % a, [P, (b - a) * PACK], BF16) for a, b in PIECES}
 
-        def weave(engine_copy, a, b):
-            engine_copy(
-                out=z_grouped[a][:].rearrange("p (c e t) -> p c t e", e=4, t=PACK),
-                in_=z[:, :, a:b].rearrange("p t (c e) -> p c t e", e=4),
+        def weave(piece, a, b):
+            nc.vector.tensor_copy(
+                out=z_grouped[piece][:, (a - piece) * PACK : (b - piece) * PACK].rearrange("p (c e t) -> p c t e", e=4, t=PACK),
+                in_=z[:, :, a - TURNED : b - TURNED].rearrange("p t (c e) -> p c t e", e=4),
+            )
+
+        by_cell = {}
+        for u in range(2):
+            for i, (first, last) in enumerate(spans):
+                by_cell[(u, i)] = sb("by_cell%d%d" % (u, i), [P, (last - first) * 2 * P], BF16)
+                nc.scalar.copy(
+                    out=by_cell[(u, i)][:].rearrange("p (b m e) -> p b m e", m=P, e=2),
+                    in_=sum_banks[(u, i)][:].rearrange("p (b e m) -> p b m e", m=P, e=2),
+                )
+        for i, (first, last) in enumerate(spans):
+            cells = (last - first) * P
+            back = bank("back_bank%d" % i, 4 + i, 2 * cells)
+            for u in (1, 0):
+                for block in range(last - first):
+                    words = by_cell[(u, i)][:].bitcast(F32)[:, block * P : (block + 1) * P]
+                    nc.tensor.transpose(back[:, u * cells + block * P : u * cells + (block + 1) * P], words, identity[:])
+            nc.scalar.copy(
+                out=z_grouped[first * P][:].bitcast(F32)[:, : 2 * cells].rearrange("p (c u) -> p c u", u=2),
+                in_=back[:].rearrange("p (u c) -> p c u", u=2),
             )
 
         def second_product(i, number, engine_copy):
@@ -211,11 +258,10 @@ def tile_picked_unet_gelu_p_kernel(
             engine_copy(out=result[:], in_=acc[:])
             nc.sync.dma_start(out=out[:, a:b], in_=result[:])
 
-        weave(nc.scalar.copy, *PIECES[0])
-        weave(nc.scalar.copy, *PIECES[1])
-        weave(nc.vector.tensor_copy, *PIECES[2])
-        second_product(0, 7, nc.scalar.copy)
-        weave(nc.vector.tensor_copy, *PIECES[3])
-        second_product(2, 0, nc.scalar.copy)
-        second_product(3, 1, nc.scalar.copy)
-        second_product(1, 2, nc.vector.tensor_copy)
+        weave(512, 512, 768)
+        weave(768, 768, U)
+        second_product(2, 4, nc.scalar.copy)
+        weave(256, TURNED, 512)
+        second_product(3, 5, nc.scalar.copy)
+        second_product(0, 6, nc.scalar.copy)
+        second_product(1, 7, nc.vector.tensor_copy)

@@ -77,11 +77,9 @@ def tile_picked_unet_gelu_p_kernel(
         x_table.append(load_x(1))
         nc.sync.dma_start(cell_sb[:], cell)
         skip_by_slot = skip.rearrange("(m t) v -> m t v", t=PACK)
-        skip_sb = []
-        for t in range(PACK):
-            plane = sb("skip%d" % t, [P, U], F32)
-            nc.sync.dma_start(out=plane[:], in_=skip_by_slot[:, t, :])
-            skip_sb.append(plane)
+        skip_sb = [sb("skip%d" % t, [P, U], F32) for t in range(PACK)]
+        for t in (0, 2, 1, 3):
+            nc.sync.dma_start(out=skip_sb[t][:], in_=skip_by_slot[:, t, :])
         w2_codes = sb("w2_codes", [P, N], I32)
         nc.sync.dma_start(out=w2_codes[:], in_=w2_words[0].rearrange("p n t -> p (n t)").bitcast(I32))
         w2_plane = sb("w2_plane", [P, N], U8)
@@ -206,8 +204,8 @@ def tile_picked_unet_gelu_p_kernel(
             engine.tensor_tensor(z[:, t, a - TURNED : b - TURNED], up[t][:, a:b], skip_sb[t][:, a:b], ADD)
 
         add_skip(nc.gpsimd, 0, TURNED, U)
-        add_skip(nc.gpsimd, 1, 512, U)
-        add_skip(nc.vector, 1, TURNED, 512)
+        add_skip(nc.gpsimd, 1, 640, U)
+        add_skip(nc.vector, 1, TURNED, 640)
         add_skip(nc.vector, 2, TURNED, U)
         add_skip(nc.vector, 3, 512, 768)
         add_skip(nc.vector, 3, 768, U)
@@ -232,7 +230,7 @@ def tile_picked_unet_gelu_p_kernel(
         for i, (first, last) in enumerate(spans):
             cells = (last - first) * P
             back = bank("back_bank%d" % i, 4 + i, 2 * cells)
-            for u in (1, 0):
+            for u in range(2):
                 for block in range(last - first):
                     words = by_cell[(u, i)][:].bitcast(F32)[:, block * P : (block + 1) * P]
                     nc.tensor.transpose(back[:, u * cells + block * P : u * cells + (block + 1) * P], words, identity[:])

@@ -204,8 +204,7 @@ def tile_picked_unet_gelu_p_kernel(
             engine.tensor_tensor(z[:, t, a - TURNED : b - TURNED], up[t][:, a:b], skip_sb[t][:, a:b], ADD)
 
         add_skip(nc.gpsimd, 0, TURNED, U)
-        add_skip(nc.gpsimd, 1, 640, U)
-        add_skip(nc.vector, 1, TURNED, 640)
+        add_skip(nc.gpsimd, 1, TURNED, U)
         add_skip(nc.vector, 2, TURNED, U)
         add_skip(nc.vector, 3, 512, 768)
         add_skip(nc.vector, 3, 768, U)

@@ -38,7 +38,7 @@ def tile_picked_unet_gelu_p_kernel(
         psum = ctx.enter_context(tc.psum_pool(name="psum", bufs=1))
 
         def sb(name, shape, dtype, tag=None):
-            return keep.tile(shape, dtype, name=name, tag=tag or name, align_bytes=64)
+            return keep.tile(shape, dtype, name=name, tag=tag or name, align_bytes=256)
 
         def bank(name, number, width):
             return psum.tile([P, width], F32, name=name, tag="bank%d" % number)

@@ -25,7 +25,8 @@ LIST_ROWS = 16
 HALF = S // 2
 QUARTER = S // 4
 PIECES = [(0, 256), (256, 512), (512, 768), (768, U)]
-EARLY = 6
+EARLY = 7
+SHIFT = 64
 TURNED = 3 * P
 
 
@@ -131,35 +132,51 @@ def tile_picked_unet_gelu_p_kernel(
         nc.vector.tensor_copy(x_plane[:], x_scale_table[:].indirect(offs_sb[:]))
         prepare_w1(1)
 
-        def first_product(acc, t, g, a, b, start):
+        def first_product(acc, t, g, a, b, start, stop):
             codes, plane = w1_codes[g], w1_plane[g]
             nc.tensor.matmul_mx(
-                out=acc[:],
+                out=acc,
                 lhsT=codes[:, t * P : (t + 1) * P].bitcast(FP8X4),
                 lhsT_scale=plane[:, t * P : (t + 1) * P],
                 rhs=x_codes[g][:, a:b].bitcast(FP8X4),
                 rhs_scale=x_plane[4 * g : P, a:b],
                 start=start,
-                stop=not start,
+                stop=stop,
             )
 
-        parts = [(0, 0, QUARTER), (1, 0, HALF), (0, QUARTER, HALF), (3, 0, HALF), (0, HALF, S), (2, 0, S), (1, HALF, S), (3, HALF, S)]
-        banks = [bank("h_bank%d" % i, i, b - a) for i, (t, a, b) in enumerate(parts)]
-        for i, (t, a, b) in enumerate(parts[:EARLY]):
-            first_product(banks[i], t, 0, a, b, True)
+        groups = [
+            [(0, 0, QUARTER)],
+            [(1, 0, HALF)],
+            [(0, QUARTER, HALF)],
+            [(1, HALF, 3 * QUARTER)],
+            [(3, 0, HALF)],
+            [(0, HALF, S)],
+            [(2, 0, S)],
+            [(1, 3 * QUARTER, S), (3, HALF, S)],
+        ]
+        banks = [bank("h_bank%d" % i, i, sum(b - a for t, a, b in group)) for i, group in enumerate(groups)]
+
+        def group_pass(i, g, opens):
+            column = 0
+            for n, (t, a, b) in enumerate(groups[i]):
+                first_product(banks[i][:, column : column + b - a], t, g, a, b, opens and n == 0, not opens and n == len(groups[i]) - 1)
+                column = column + b - a
+
+        for i in range(EARLY):
+            group_pass(i, 0, True)
         for a, b in ((0, QUARTER), (QUARTER, HALF), (HALF, S)):
             nc.vector.tensor_copy(x_codes[1][:, a:b], x_table[1][:].bitcast(U32).indirect(entries(offs_sb, a, b)))
-        for i, (t, a, b) in enumerate(parts):
-            first_product(banks[i], t, 1, a, b, i >= EARLY)
-        for i, (t, a, b) in enumerate(parts):
-            if i >= EARLY:
-                first_product(banks[i], t, 0, a, b, False)
+        for i in range(len(groups)):
+            group_pass(i, 1, i >= EARLY)
+        for i in range(EARLY, len(groups)):
+            group_pass(i, 0, False)
 
         h = [sb("h%d" % t, [P, S], F32) for t in range(PACK)]
 
-        def gelu(i):
-            t, a, b = parts[i]
-            nc.scalar.activation(h[t][:, a:b], banks[i][:], GELU)
+        def gelu(i, n):
+            column = sum(b - a for t, a, b in groups[i][:n])
+            t, a, b = groups[i][n]
+            nc.scalar.activation(h[t][:, a:b], banks[i][:, column : column + b - a], GELU)
 
         def scatter_vector(t, a, b):
             nc.vector.tensor_copy(up[t][:].indirect(entries(cell_sb, a, b)), h[t][:, a:b])
@@ -167,15 +184,16 @@ def tile_picked_unet_gelu_p_kernel(
         def scatter_scalar(t, a, b):
             nc.scalar.activation(up[t][:].indirect(entries(cell_sb, a, b)), h[t][:, a:b], COPY)
 
-        for i in range(6):
-            gelu(i)
-        for t, split in ((0, QUARTER), (1, HALF), (3, HALF), (2, S)):
-            scatter_vector(t, 0, split)
-        scatter_scalar(0, QUARTER, S)
-        gelu(6)
-        gelu(7)
-        scatter_scalar(1, HALF, S)
-        scatter_scalar(3, HALF, S)
+        for i in range(EARLY):
+            gelu(i, 0)
+        shares = (QUARTER, HALF + SHIFT, S, HALF - SHIFT)
+        for t in (0, 1, 3, 2):
+            scatter_vector(t, 0, shares[t])
+        scatter_scalar(0, shares[0], S)
+        gelu(EARLY, 0)
+        scatter_scalar(1, shares[1], S)
+        gelu(EARLY, 1)
+        scatter_scalar(3, shares[3], S)
 
         spans = [(0, 2), (2, 3)]
         sum_banks = {(u, i): bank("sum_bank%d%d" % (u, i), 2 * u + i, (b - a) * 2 * P) for u in range(2) for i, (a, b) in enumerate(spans)}

from contextlib import ExitStack

import concourse.mybir as mybir
from concourse.masks import make_identity

K, T, S, H, N, U = 1024, 2048, 512, 512, 128, 1024
FLOPS = 2 * K * H * S + 2 * H * N * U

F32 = mybir.dt.float32
BF16 = mybir.dt.bfloat16
I32 = mybir.dt.int32
U32 = mybir.dt.uint32
U16 = mybir.dt.uint16
U8 = mybir.dt.uint8
FP8X4 = mybir.dt.float8_e4m3fn_x4
GELU = mybir.ActivationFunctionType.Gelu_apprx_tanh
COPY = mybir.ActivationFunctionType.Copy
ADD = mybir.AluOpType.add

P = 128
PACK = 4
K_PASS = P * PACK
PASSES = K // K_PASS
LIST_ROWS = 16
HALF = S // 2
QUARTER = S // 4
PIECES = [(0, 256), (256, 512), (512, 768), (768, U)]
EARLY = 7
SHIFT = 64
TURNED = 3 * P


def tile_picked_unet_gelu_p_kernel(
    tc, x_words, x_scales, w1, w2_words, w2_scales, skip, offs, cell, out
):
    nc = tc.nc
    with ExitStack() as ctx:
        keep = ctx.enter_context(tc.tile_pool(name="keep", bufs=1))
        psum = ctx.enter_context(tc.psum_pool(name="psum", bufs=1))

        def sb(name, shape, dtype, tag=None):
            return keep.tile(shape, dtype, name=name, tag=tag or name, align_bytes=256)

        def bank(name, number, width):
            return psum.tile([P, width], F32, name=name, tag="bank%d" % number)

        def entries(tile, a, b):
            return tile[:, a // LIST_ROWS : b // LIST_ROWS]

        offs_sb = keep.tile([P, S // LIST_ROWS], U16, name="offs_sb")
        cell_sb = keep.tile([P, S // LIST_ROWS], U16, name="cell_sb")

        x_scale_table = sb("x_scale_table", [P, T], U8)
        nc.gpsimd.memset(x_scale_table[:].bitcast(I32), 0)

        def load_x(g):
            table = sb("x_table%d" % g, [P, T], I32)
            nc.sync.dma_start(out=table[:], in_=x_words[g].rearrange("p n t -> p (n t)").bitcast(I32))
            return table

        w1_raw = [sb("w1_raw%d" % g, [P, PACK, H], F32) for g in range(PASSES)]

        def load_w1(g, first, last):
            rows = w1[g * K_PASS : (g + 1) * K_PASS, :].rearrange("(p j) c -> p j c", j=PACK)
            nc.sync.dma_start(out=w1_raw[g][:, first:last, :], in_=rows[:, first:last, :])

        def load_x_scales(first):
            for r, g in ((first, 0), (first, 1), (first + 1, 0), (first + 1, 1)):
                nc.sync.dma_start(out=x_scale_table[4 * g + r : P : 32, :].bitcast(I32), in_=x_scales[g, r:16:4, :].bitcast(I32))

        load_w1(0, 0, 2)
        nc.sync.dma_start(offs_sb[:], offs)
        load_x_scales(0)
        load_w1(0, 2, PACK)
        x_table = [load_x(0)]
        load_x_scales(2)
        load_w1(1, 0, PACK)
        x_table.append(load_x(1))
        nc.sync.dma_start(cell_sb[:], cell)
        skip_by_slot = skip.rearrange("(m t) v -> m t v", t=PACK)
        skip_sb = [sb("skip%d" % t, [P, U], F32) for t in range(PACK)]
        for t in (0, 2, 1, 3):
            nc.sync.dma_start(out=skip_sb[t][:], in_=skip_by_slot[:, t, :])
        w2_codes = sb("w2_codes", [P, N], I32)
        nc.sync.dma_start(out=w2_codes[:], in_=w2_words[0].rearrange("p n t -> p (n t)").bitcast(I32))
        w2_plane = sb("w2_plane", [P, N], U8)
        nc.vector.memset(w2_plane[:].bitcast(I32), 0)
        for r in range(4):
            nc.sync.dma_start(out=w2_plane[r:P:32, :].bitcast(I32), in_=w2_scales[0, r:16:4, :].bitcast(I32))

        up = [sb("up%d" % t, [P, U], F32) for t in range(PACK)]
        nc.vector.memset(up[1][:], 0.0)
        nc.scalar.activation(up[0][:], up[1][:], GELU)
        for t in range(2, PACK):
            nc.gpsimd.memset(up[t][:], 0.0)

        identity = sb("identity", [P, P], F32)
        make_identity(nc, identity[:])

        def quantize(name, source, width):
            codes = sb(name + "_codes", [P, width], U32)
            plane = sb(name + "_plane", [P, width], U8)
            nc.vector.quantize_mx(out=codes[:].bitcast(FP8X4), scales=plane[:], in_=source)
            return codes, plane

        w1_grouped = [sb("w1_grouped%d" % g, [P, H * PACK], BF16) for g in range(PASSES)]

        def cast_w1(engine_copy, g, first, last):
            engine_copy(
                out=w1_grouped[g][:].rearrange("p (t m j) -> p m j t", t=PACK, j=PACK)[:, :, :, first:last],
                in_=w1_raw[g][:].rearrange("p j (m t) -> p m j t", t=PACK)[:, :, :, first:last],
            )

        w1_codes = [sb("w1_codes%d" % g, [P, H], U32) for g in range(PASSES)]
        w1_plane = [sb("w1_plane%d" % g, [P, H], U8) for g in range(PASSES)]

        def prepare_w1(g):
            cast_w1(nc.vector.tensor_copy, g, 0, 2)
            cast_w1(nc.scalar.copy, g, 2, PACK)
            for first in (0, H // 2):
                nc.vector.quantize_mx(
                    out=w1_codes[g][:, first : first + H // 2].bitcast(FP8X4),
                    scales=w1_plane[g][:, first : first + H // 2],
                    in_=w1_grouped[g][:, first * PACK : (first + H // 2) * PACK],
                )

        prepare_w1(0)

        x_codes = [sb("x_codes%d" % g, [P, S], U32) for g in range(PASSES)]
        x_plane = sb("x_plane", [P, S], U8)
        nc.vector.tensor_copy(x_codes[0][:], x_table[0][:].bitcast(U32).indirect(offs_sb[:]))
        nc.vector.tensor_copy(x_plane[:], x_scale_table[:].indirect(offs_sb[:]))
        prepare_w1(1)

        def first_product(acc, t, g, a, b, start, stop):
            codes, plane = w1_codes[g], w1_plane[g]
            nc.tensor.matmul_mx(
                out=acc,
                lhsT=codes[:, t * P : (t + 1) * P].bitcast(FP8X4),
                lhsT_scale=plane[:, t * P : (t + 1) * P],
                rhs=x_codes[g][:, a:b].bitcast(FP8X4),
                rhs_scale=x_plane[4 * g : P, a:b],
                start=start,
                stop=stop,
            )

        groups = [
            [(0, 0, QUARTER)],
            [(1, 0, HALF)],
            [(0, QUARTER, HALF)],
            [(1, HALF, 3 * QUARTER)],
            [(3, 0, HALF)],
            [(0, HALF, S)],
            [(2, 0, S)],
            [(1, 3 * QUARTER, S), (3, HALF, S)],
        ]
        banks = [bank("h_bank%d" % i, i, sum(b - a for t, a, b in group)) for i, group in enumerate(groups)]

        def group_pass(i, g, opens):
            column = 0
            for n, (t, a, b) in enumerate(groups[i]):
                first_product(banks[i][:, column : column + b - a], t, g, a, b, opens and n == 0, not opens and n == len(groups[i]) - 1)
                column = column + b - a

        for i in range(EARLY):
            group_pass(i, 0, True)
        for a, b in ((0, QUARTER), (QUARTER, HALF), (HALF, S)):
            nc.vector.tensor_copy(x_codes[1][:, a:b], x_table[1][:].bitcast(U32).indirect(entries(offs_sb, a, b)))
        for i in range(len(groups)):
            group_pass(i, 1, i >= EARLY)
        for i in range(EARLY, len(groups)):
            group_pass(i, 0, False)

        h = [sb("h%d" % t, [P, S], F32) for t in range(PACK)]

        def gelu(i, n):
            column = sum(b - a for t, a, b in groups[i][:n])
            t, a, b = groups[i][n]
            nc.scalar.activation(h[t][:, a:b], banks[i][:, column : column + b - a], GELU)

        def scatter_vector(t, a, b):
            nc.vector.tensor_copy(up[t][:].indirect(entries(cell_sb, a, b)), h[t][:, a:b])

        def scatter_scalar(t, a, b):
            nc.scalar.activation(up[t][:].indirect(entries(cell_sb, a, b)), h[t][:, a:b], COPY)

        for i in range(EARLY):
            gelu(i, 0)
        shares = (QUARTER, HALF + SHIFT, S, HALF - SHIFT)
        for t in (0, 1, 3, 2):
            scatter_vector(t, 0, shares[t])
        scatter_scalar(0, shares[0], S)
        gelu(EARLY, 0)
        scatter_scalar(1, shares[1], S)
        gelu(EARLY, 1)
        scatter_scalar(3, shares[3], S)

        spans = [(0, 2), (2, 3)]
        sum_banks = {(u, i): bank("sum_bank%d%d" % (u, i), 2 * u + i, (b - a) * 2 * P) for u in range(2) for i, (a, b) in enumerate(spans)}

        def turn(source, t, opens, closes):
            for i, (first, last) in enumerate(spans):
                for block in range(first, last):
                    column = ((block - first) * 2 + t % 2) * P
                    nc.tensor.matmul(
                        sum_banks[(t // 2, i)][:, column : column + P],
                        lhsT=source[:, block * P : (block + 1) * P],
                        rhs=identity[:],
                        start=opens and block == first,
                        stop=closes and block == last - 1,
                        is_transpose=True,
                    )

        for t in range(PACK):
            turn(skip_sb[t], t, t % 2 == 0, False)
        for t in (0, 1, 2, 3):
            turn(up[t], t, False, t % 2 == 1)

        z = sb("z", [P, PACK, U - TURNED], BF16)

        def add_skip(engine, t, a, b):
            engine.tensor_tensor(z[:, t, a - TURNED : b - TURNED], up[t][:, a:b], skip_sb[t][:, a:b], ADD)

        add_skip(nc.gpsimd, 0, TURNED, U)
        add_skip(nc.gpsimd, 1, TURNED, U)
        add_skip(nc.vector, 2, TURNED, U)
        add_skip(nc.vector, 3, 512, 768)
        add_skip(nc.vector, 3, 768, U)
        add_skip(nc.vector, 3, TURNED, 512)

        z_grouped = {a: sb("z_grouped%d" % a, [P, (b - a) * PACK], BF16) for a, b in PIECES}

        def weave(piece, a, b):
            nc.vector.tensor_copy(
                out=z_grouped[piece][:, (a - piece) * PACK : (b - piece) * PACK].rearrange("p (c e t) -> p c t e", e=4, t=PACK),
                in_=z[:, :, a - TURNED : b - TURNED].rearrange("p t (c e) -> p c t e", e=4),
            )

        by_cell = {}
        for u in range(2):
            for i, (first, last) in enumerate(spans):
                by_cell[(u, i)] = sb("by_cell%d%d" % (u, i), [P, (last - first) * 2 * P], BF16)
                nc.scalar.copy(
                    out=by_cell[(u, i)][:].rearrange("p (b m e) -> p b m e", m=P, e=2),
                    in_=sum_banks[(u, i)][:].rearrange("p (b e m) -> p b m e", m=P, e=2),
                )
        for i, (first, last) in enumerate(spans):
            cells = (last - first) * P
            back = bank("back_bank%d" % i, 4 + i, 2 * cells)
            for u in range(2):
                for block in range(last - first):
                    words = by_cell[(u, i)][:].bitcast(F32)[:, block * P : (block + 1) * P]
                    nc.tensor.transpose(back[:, u * cells + block * P : u * cells + (block + 1) * P], words, identity[:])
            nc.scalar.copy(
                out=z_grouped[first * P][:].bitcast(F32)[:, : 2 * cells].rearrange("p (c u) -> p c u", u=2),
                in_=back[:].rearrange("p (u c) -> p c u", u=2),
            )

        def second_product(i, number, engine_copy):
            a, b = PIECES[i]
            z_codes, z_plane = quantize("z%d" % a, z_grouped[a][:], b - a)
            acc = bank("out_bank%d" % i, number, b - a)
            nc.tensor.matmul_mx(
                out=acc[:],
                lhsT=w2_codes[:].bitcast(FP8X4),
                lhsT_scale=w2_plane[:],
                rhs=z_codes[:].bitcast(FP8X4),
                rhs_scale=z_plane[:],
                start=True,
                stop=True,
            )
            result = sb("result%d" % a, [P, b - a], F32)
            engine_copy(out=result[:], in_=acc[:])
            nc.sync.dma_start(out=out[:, a:b], in_=result[:])

        weave(512, 512, 768)
        weave(768, 768, U)
        second_product(2, 4, nc.scalar.copy)
        weave(256, TURNED, 512)
        second_product(3, 5, nc.scalar.copy)
        second_product(0, 6, nc.scalar.copy)
        second_product(1, 7, nc.vector.tensor_copy)
